import numpy as np, ml_dtypes
CORES = [13,21,141,149]
N = 4
BF = ml_dtypes.bfloat16
V, H, M, CAP, R = 1280, 80, 2, 32, 4
L = M * H
def lanes(t, r):
    c = (M * (N * t + r) + np.arange(M)) & 15
    return (16 * np.arange(H)[None, :] + c[:, None]).reshape(-1)
def pack(b, x, lm):
    return {"nb": np.ascontiguousarray(b.reshape(N, 128, V)).astype(np.float32), "xs": np.ascontiguousarray(x.reshape(N, 128, V)).astype(np.float32).astype(BF),
            "lim": np.ascontiguousarray(lm.reshape(N, 128, 1)).astype(np.int32)}
def parts(rng):
    dens = rng.choice(np.array([0.08, 0.25, 0.5, 0.8]), (N, 8, 1, V)); u = rng.random((N, 8, 16, V))
    h = np.minimum((V * u * u).astype(np.int64), V - 1)
    pool = rng.integers(V // 4, V, (8, 12)); known = pool[np.arange(8)[None, :, None, None], rng.integers(0, 12, (N, 8, 16, V))]
    h = np.where(rng.random((N, 8, 16, V)) < 0.35, known, h)
    b = np.where(rng.random((N, 8, 16, V)) < dens, h, V)
    top = np.where(rng.random((N, 8, 1, V)) < 0.02, 256, rng.choice(np.array([4, 16, 40, 64]), (N, 8, 1, V)))
    x = (top * rng.random((N, 8, 16, V))).astype(np.int64)
    lm = rng.permutation(np.array([6, 16, 28, 45, 70, 110, 180, 300]))[None, :, None] + rng.integers(0, 8, (N, 8, 16))
    return b, x, lm
def late(rng, b, x, lm, g):
    E = np.stack([np.append(rng.permutation(lanes(0, r)[:-1]), lanes(0, r)[-1])[-26:] for r in range(N)])
    C = np.stack([np.append(rng.permutation(lanes(1, r)[:-1]), lanes(1, r)[-1])[-14:] for r in range(N)])
    D = np.stack([rng.permutation(np.setdiff1d(lanes(2, r), E[r]))[:4] for r in range(N)])
    low = E[:, :12]; own = E[:, 12:18]; top = E[:, 18:]; lows = low.reshape(-1)
    pool = np.setdiff1d(np.arange(V), np.concatenate([E.reshape(-1), C.reshape(-1), D.reshape(-1)]))
    b[:, g] = rng.choice(pool, (N, 16, V)); x[:, g] = rng.integers(128, 256, (N, 16, V)); lm[:, g] = rng.integers(600, 1600, (N, 16))
    for r in range(N):
        b[r, g][:, E[r]] = V; b[r, g][:, C[r, :3]] = V
    for r in range(N):
        z = rng.permutation(pool)[:12]; x[r, g][:, z] = 255; x[r, g][rng.integers(0, 16, 12), z] = 254
        b[r, g][rng.integers(0, 16, 12), low[r]] = z
        p = rng.integers(0, 16, 8); b[r, g][p, top[r]] = rng.choice(pool, 8); b[r, g][(p + rng.integers(1, 16, 8)) & 15, top[r]] = rng.choice(pool, 8)
        q = (r + 1) % N; s = C[r, :6]; k = rng.integers(0, 16, 6); j = (k + rng.integers(1, 16, 6)) & 15
        b[q, g][k, own[q]] = s; b[r, g][k, s] = s; b[r, g][j, s] = own[q]
        for i in range(8):
            n = rng.permutation(lows)[:16]; n[12 + (i & 3)] = top[q, i] if i < 4 else top[0, i]
            b[r, g][:, C[r, 6 + i]] = n
        if r < N - 1:
            for i in range(4):
                n = rng.permutation(lows)[:16]; n[int(rng.integers(0, 16))] = top[0, 4 + i]
                b[r, g][:, D[r, i]] = n
def setup_inputs(rng):
    return pack(*parts(rng))
def setup_inputs_spread(rng):
    d = rng.random((N, 8, 1, V))
    b = np.where(rng.random((N, 8, 16, V)) < d * d * d, rng.integers(0, V, (N, 8, 16, V)), V)
    x = np.minimum((np.exp2(8 * rng.random((N, 8, 1, V))) * rng.random((N, 8, 16, V))).astype(np.int64), 255)
    lm = np.minimum((np.exp2(3 + 9 * rng.random((N, 8, 1))) * (0.5 + 0.5 * rng.random((N, 8, 16)))).astype(np.int64), 4079)
    return pack(b, x, lm)
def setup_inputs_ends(rng):
    x = 255 * np.where(rng.random((N, 8, 1, V)) < 0.5, rng.integers(0, 2, (N, 8, 1, V)), rng.integers(0, 2, (N, 8, 16, V)))
    x[:, 1::2, :, :16] = 255; x[:, 1::2, :, V - 1] = 255
    mode = rng.choice(np.array([0, 0, 1, 2, 2, 2, 3, 4]), (N, 8, 1, V)); coin = rng.integers(0, 2, (N, 8, 16, V))
    v = np.arange(V)[None, :]; p = np.arange(16)[:, None]
    b = np.where(mode == 0, 0, np.where(mode == 1, V, np.where(mode == 2, coin * V, np.where(mode == 3, np.where(coin == 1, p, V - 1), rng.integers(0, V + 1, (N, 8, 16, V))))))
    b[:, 0:6:2, :, 0:16:2] = V
    b[:, 3:6:2, :, 0:16] = V; b[:, 3:6:2, 5, 0:16] = 0
    b[N - 1, 7] = np.where((v >= V - 192) & (p == ((v >> 4) & 15)), V, 0)
    big = np.array([9, 16, 8, 16, 0, 9, 12, 16])[None, :, None]
    lm = np.where(np.argsort(rng.random((N, 8, 16)), axis=2) < big, 4079, 0)
    return pack(b, x, lm)
def setup_inputs_corners(rng):
    x = rng.integers(16, 32, (N, 8, 16, V)); x[..., V - 80:V - 16] = 255; x[..., V - 16:] = 0
    pos = np.argsort(rng.random((N, 8, 16, V)), axis=2)
    many = np.where((rng.random((N, 8, 16, V)) < 0.4) | (pos < 4), rng.integers(0, V - 16, (N, 8, 16, V)), V)
    one = np.where(pos == 0, rng.integers(0, V - 80, (N, 8, 16, V)), V)
    kind = rng.choice(np.array([0, 1, 2, 2]), (N, 8, 1, V)); counts = (CAP, CAP + 1, L, CAP - 1, 1, 0, CAP, 2)
    for q in range(N):
        v = lanes(0, q)
        for g in range(8):
            n = counts[(g + 3 * q) % 8]; o = rng.permutation(L)
            kind[q, g, 0, v[o[:n]]] = 0 if g % 4 == 2 else rng.integers(0, 2, n)
            kind[q, g, 0, v[o[n:]]] = rng.integers(1, 3, L - n) if g % 4 == 2 else 2
    b = np.where(kind == 0, V, np.where(kind == 1, one, many))
    lm = 40 + rng.integers(0, 8, (N, 8, 16)); o = np.argsort(rng.random((N, 8, 16)), axis=2)
    lm[:, 1::2] = np.where(o[:, 1::2] < 9, lm[:, 1::2], 0); lm[:, 2::4] = np.where(o[:, 2::4] < 8, lm[:, 2::4], 0)
    return pack(b, x, lm)
def setup_inputs_crowd(rng):
    b, x, lm = parts(rng)
    b[:, :4] = np.where(rng.random((N, 4, 16, V)) < 0.1, rng.integers(V - 128, V, (N, 4, 16, V)), V); b[:, :4, 0, :] = 0
    v = np.arange(V)
    for t in range(16 // (N * M)):
        c = (M * (N * t + N - 1)) & 15
        b[:, 1:4:2, 0, np.flatnonzero(((v & 15) == c) & ((v >> 4) % CAP == CAP - 1))] = V
    lm[:, :4] = 4079; x[:, :2] = 255
    b[:, 4:] = np.where(b[:, 4:] < V, rng.choice(np.array([0, 1, 18, 40, V - 1]), (N, 4, 16, V)), V); b[:, 4:, :, :48] = V
    return pack(b, x, lm)
def setup_inputs_alike(rng):
    b, x, lm = parts(rng)
    u = rng.random((N, 8, 3, V)); few = np.minimum((V * u * u).astype(np.int64), V - 1)
    few[:, :, 0] = np.where(rng.random((N, 8, V)) < 0.15, np.arange(V), few[:, :, 0])
    pool = rng.integers(V // 2, V, (8, 4)); few[:, :, 2] = pool[np.arange(8)[None, :, None], rng.integers(0, 4, (N, 8, V))]
    which = np.minimum(rng.integers(0, 3, (N, 8, 16, V)), rng.integers(0, 3, (N, 8, 1, V)))
    b = np.where(rng.random((N, 8, 16, V)) < rng.choice(np.array([0.4, 0.8, 1.0]), (N, 8, 1, V)), np.take_along_axis(few, which, 2), V)
    lm = np.minimum(4 * lm, 4079)
    late(rng, b, x, lm, int(rng.integers(0, 8)))
    return pack(b, x, lm)
def check_inputs(d):
    bad = []
    for k, lo, hi in (("nb", 0, V), ("xs", 0, 255), ("lim", 0, 4079)):
        a = np.asarray(d[k]).astype(np.float64)
        if not np.all((a >= lo) & (a <= hi)): bad.append("range of " + k)
        elif not np.all(a == np.floor(a)): bad.append("whole numbers in " + k)
    return bad
def reference(nb, xs, lim):
    b = nb.astype(np.int32).reshape(N, 8, 16, V); x = xs.astype(np.float32).astype(np.int32).reshape(N, 8, 16, V)
    lm = lim.astype(np.int64).reshape(N, 8, 16, 1)
    J = np.tile(np.arange(V), (8, 1)); gone = np.zeros((8, V), bool)
    A = [0] * N; g8 = np.arange(8)[:, None, None]
    for t in range(R):
        new = []
        for r in range(N):
            v = lanes(t, r); q = b[r][:, :, v]
            has = q < V; u = np.where(has, q, 0)
            n = J[g8, u]; elem = has & gone[g8, u]; var = has & ~elem
            at = n.reshape(8, 1, 16 * L)
            Q = np.take_along_axis(b[r], at, 2).reshape(8, 16, 16, L); X = np.take_along_axis(x[r], at, 2).reshape(8, 16, 16, L)
            ek = elem[:, None]
            cov = var & np.any((Q == q[:, :, None, :]) & ek, axis=2)
            unc = var & ~cov
            deg = np.sum(np.where(unc[:, None], X, 0), axis=2) + np.max(np.where(ek, X, 0), axis=2)
            live = ~gone[:, v]
            hit = live & (np.sum(deg <= lm[r] + (A[r] & 7), axis=1) >= 9)
            piv = hit & (np.add.accumulate(hit.astype(np.int64), axis=1) <= CAP)
            col = np.minimum(np.where(unc & (q != v), q, V), np.min(np.where(ek & (Q != v), Q, V), axis=2))
            S = np.where(elem, np.sum(X, axis=1), -1); k = np.argmax(S, axis=1)
            e = np.take_along_axis(n, k[:, None, :], 1)[:, 0, :]
            b[r][:, :, v] = np.where(cov & (live & ~piv)[:, None, :], V, q)
            new.append((v, piv, col, np.minimum(deg, 255), e, piv & np.any(elem, axis=1)))
        for g in range(8):
            es = []; vs = []
            for v, piv, col, sz, e, cl in new:
                w = np.flatnonzero(piv[g]); b[:, g][:, :, v[w]] = col[g][:, w]; x[:, g][:, :, v[w]] = sz[g][:, w]; gone[g, v[w]] = True
                w = np.flatnonzero(cl[g]); es.append(e[g][w]); vs.append(v[w])
            ue, ui = np.unique(np.concatenate(es), return_index=True)
            J[g, ue] = np.concatenate(vs)[ui]
            J[g] = J[g][J[g]]
        A = [int(np.sum(a[1])) for a in new]
    return {"yn": b.reshape(N, 128, V).astype(np.float32), "yx": x.reshape(N, 128, V).astype(np.float32).astype(BF), "yj": np.stack([J] * N).astype(np.float32)}

@@ -1,0 +1,667 @@
+from concourse.bass import DstId, RemoteDMATransfer
+from concourse.mybir import AluOpType as Op, ActivationFunctionType as Fn
+
+V, H, CAP, ROUNDS = 1280, 80, 32, 4
+N = 4
+L = 2 * H
+LX = L + CAP
+VT = 1792
+G0 = 1288
+BL = 36
+IDW = 640
+SHIFT = 512 * 32618
+FP, BF, I32, U16 = "float32", "bfloat16", "int32", "uint16"
+CH0 = [(0, 64), (64, 160)]
+CH = [(0, 64), (64, 128), (128, 160)]
+
+_S = {
+    "nm": (VT, FP), "en": (VT, FP), "rs": (VT, FP), "vn": (G0, FP), "jt": (VT, FP), "xm": (VT, BF), "xo": (VT, BF),
+    "la": (576, FP), "ln": (576, FP), "w": (IDW, FP), "vid": (IDW, FP), "vb": (128, FP), "idc": (512, FP),
+    "jwa": (32, U16), "jwb": (32, U16), "jwc": (32, U16), "evu": (32, U16), "cwu": (32, U16), "jwf": (32, FP),
+    "qf0": (LX, FP), "qf1": (LX, FP), "qu0": (L, U16), "qu1": (L, U16), "qr0": (16 * L, FP), "qr1": (16 * L, FP),
+    "lv0": (LX, FP), "lv1": (LX, FP), "ns0": (LX, FP), "ns1": (LX, FP), "dead0": (L, BF), "dead1": (L, BF),
+    "xg": (16 * L, BF), "eq": (16 * L, BF), "xv": (16 * L, BF), "msc": (16 * L, BF), "lmx": (L, FP), "deg": (LX, FP),
+    "ocx": (LX, FP), "e1": (LX, FP), "esg": (L, FP), "q2": (L, FP), "q3": (L, FP), "qn": (L, U16), "ok": (L, BF), "hit": (LX, BF),
+    "cum": (LX, BF), "c255": (LX, BF), "sg": (2 * LX, BF), "pla": (2, FP), "plw": (2, U16), "vx": (2, FP), "vy": (2, FP),
+    "piv": (L, BF),
+    "qp": (32, U16), "vp": (32, U16), "e1p": (32, FP), "ocp": (32, FP), "ocq": (32, FP), "xgp": (512, BF), "slg": (512, FP),
+    "xn": (512, FP), "vr": (512, FP), "cc": (512, FP), "nsc": (512, FP), "key": (512, FP), "ksc": (512, FP),
+    "mi": (32, I32), "mj": (32, I32), "kd": (32, FP),
+    "kw": (32, FP), "ke": (64, FP), "kf": (64, FP), "kg": (64, FP), "jd": (256, FP), "js": (256, FP), "jr": (256, FP), "xr": (256, FP),
+    "er": (256, FP), "jf": (384, FP), "xt": (128, FP), "nt": (128, FP), "a1": (1, BF), "ai": (1, I32), "aj": (1, I32),
+    "limi": (1, I32), "limf": (1, FP), "lima": (1, FP), "limb": (1, FP), "c32c": (1, FP), "c1280": (1, FP), "mbig": (1, FP),
+    "neg1": (1, FP), "half": (1, FP),
+    "one": (128, BF), "idn": (128, BF), "i1280": (128, BF), "idead": (128, BF), "ipen": (128, BF), "bd": (128, BF), "bd8": (128, BF),
+    "dk": (2048, BF), "o16": (128, BF), "pii": (1, I32), "pij": (2, I32), "p15": (1, FP), "pg": (1, FP), "sh": (2, FP), "sc": (2, FP),
+    "dmp": (2, FP), "col": (512, I32), "cki": (512, I32), "gi": (128, I32), "dg": (256, FP), "seg": (1024, BF),
+    "c32": (64, I32), "seg32": (64, BF), "kb": (512, FP), "kp": (512, BF), "tri": (64, FP), "lrep": (L, U16),
+}
+PSUM = ["b0", "b1", "b2", "bdeg", "bhit", "bkey", "bself"]
+SCRATCH = {n: ("sbuf", [128, c], d) for n, (c, d) in _S.items()}
+SCRATCH.update({n: ("psum", [128, 512], FP) for n in PSUM})
+SEMAPHORES = (["qv", "qs", "qt", "qg", "dn", "dx", "do", "dl", "on", "ox", "oj", "loc"]
+              + ["a%d" % b for b in range(16)] + ["n%d" % b for b in range(16)])
+
+
+def plan(core, T, topo):
+    direct = [d for d in T.cores if d != core and topo.may_write(core, d)]
+    rest = [d for d in T.cores if d != core and not topo.may_write(core, d)]
+    relays = []
+    for d in rest:
+        ok = [x for x in topo.cores_of(core) if x not in T.cores and x not in relays and topo.may_write(x, d)]
+        ok.sort(key=lambda x: (topo.die(x) != topo.die(core), x))
+        relays.append(ok[0])
+    return direct, list(zip(relays, rest))
+
+
+def bits(engines):
+    return sum(1 << e for e in engines)
+
+
+def groups(t):
+    a, n = ("la", "a"), ("ln", "n")
+    return [[a, n]] if t == 0 else [[a], [n]] if t < ROUNDS - 1 else [[n], [a]]
+
+
+def share(engines, n, i):
+    k = len(engines) // n
+    return engines[i * k:(i + 1) * k]
+
+
+def legs(core, T, topo, m):
+    direct, via = plan(core, T, topo)
+    relays = [x for x, d in via]
+    return [[(d, j, share(topo.engines(core, d), len(ds) * m, i * m + j)) for i, d in enumerate(ds) for j in range(m)]
+            for ds in (relays, direct)]
+
+
+def onward(x, dst, topo, m):
+    return [(j, share(topo.engines(x, dst), m, j)) for j in range(m)]
+
+
+def relay_program(g, core, T, topo):
+    for r, src in enumerate(T.cores):
+        for x, dst in plan(src, T, topo)[1]:
+            if x != core:
+                continue
+            rid, pid = topo.addr(dst, core)
+            n = 0
+            for t in range(ROUNDS):
+                b = 4 * t + r
+                for grp in groups(t):
+                    for call in legs(src, T, topo, len(grp)):
+                        for d, j, eng in call:
+                            if d == core:
+                                g.wait_ge(T.sem["%s%d" % (grp[j][1], b)], len(eng))
+                    tr = []
+                    for j, eng in onward(core, dst, topo, len(grp)):
+                        piece = T[grp[j][0]][:, BL * b:BL * (b + 1)]
+                        tr.append(RemoteDMATransfer(dst_ids=[DstId(rid=rid, pnc=pid)], dma_engine_mask=bits(eng),
+                                                    remote_sem=T.sem["%s%d" % (grp[j][1], b)], srcs=[piece], dsts=[piece]))
+                        n += len(eng)
+                    g.remote_dma_fused(tr, local_sem=T.sem.loc)
+            g.wait_ge(T.sem.loc, n)
+
+
+def rank_program(g, core, T, topo):
+    rank = T.rank_of(core)
+    if rank is None:
+        relay_program(g, core, T, topo)
+        return
+    r = rank
+    Q = {"v": g.vector, "s": g.scalar, "t": g.tensor, "g": g, "y": g.sync}
+    cnt = {q: 0 for q in "vstg"}
+    known = {q: {} for q in "vstgy"}
+    hist = {}
+    totals = {}
+
+    def is_psum(n):
+        return n in PSUM
+
+    def deps(q, reads, writes):
+        toks = []
+        for kind, regs in (("r", reads), ("w", writes)):
+            for n, lo, hi in regs:
+                for e in hist.get(n, ()):
+                    if not is_psum(n) and (e[1] <= lo or hi <= e[0]):
+                        continue
+                    if kind == "r" and e[2] == "r" and not is_psum(n):
+                        continue
+                    if is_psum(n) and e[3] == q and (q == "t" or kind == "r" and e[2] == "r"):
+                        continue
+                    toks.append((e[4], e[5], e[6]))
+        return toks
+
+    def wait_for(q, toks):
+        need = {}
+        k = known[q]
+        for s, v, snap in toks:
+            if need.get(s, (0, None))[0] < v:
+                need[s] = (v, snap)
+        for s in list(need):
+            v = need[s][0]
+            if k.get(s, 0) >= v or any(o != s and sn.get(s, 0) >= v and k.get(o, 0) < ov for o, (ov, sn) in need.items()):
+                continue
+            Q[q].wait_ge(T.sem[s], v)
+        for s, (v, snap) in need.items():
+            k[s] = max(k.get(s, 0), v)
+            for o, ov in snap.items():
+                k[o] = max(k.get(o, 0), ov)
+
+    def note(q, reads, writes, sem, val, snap):
+        for n, lo, hi in writes:
+            h = hist.setdefault(n, [])
+            h[:] = [e for e in h if not (lo <= e[0] and e[1] <= hi)]
+            h.append((lo, hi, "w", q, sem, val, snap))
+        for n, lo, hi in reads:
+            h = hist.setdefault(n, [])
+            h[:] = [e for e in h if not (e[2] == "r" and e[3] == q and q in cnt and lo <= e[0] and e[1] <= hi)]
+            h.append((lo, hi, "r", q, sem, val, snap))
+
+    def flat(x):
+        if not isinstance(x, tuple):
+            return []
+        if x[0] == "I":
+            return flat(x[1]) + flat(x[2])
+        return [(x[0], x[1], x[2])]
+
+    def ap(x):
+        if not isinstance(x, tuple):
+            return x
+        if x[0] == "I":
+            return ap(x[1]).indirect(ap(x[2]))
+        if len(x) > 3:
+            return T[x[0]][:, x[1]:x[2]:x[3]]
+        return T[x[0]][:, x[1]:x[2]]
+
+    def emit(q, fn, outs, ins):
+        reads, writes = [], []
+        for x in ins:
+            reads += flat(x)
+        for x in outs:
+            if isinstance(x, tuple) and x[0] == "I":
+                writes += flat(x[1])
+                reads += flat(x[2])
+            else:
+                writes += flat(x)
+        wait_for(q, deps(q, reads, writes))
+        inst = fn()
+        sem = "q" + q
+        cnt[q] += 1
+        inst.then_inc(T.sem[sem], 1)
+        totals[sem] = cnt[q]
+        snap = dict(known[q])
+        snap[sem] = cnt[q]
+        note(q, reads, writes, sem, cnt[q], snap)
+
+    def tc(out, in_):
+        emit("v", lambda: g.vector.tensor_copy(out=ap(out), in_=ap(in_)), [out], [in_])
+
+    def tt(out, a, b, op):
+        emit("v", lambda: g.vector.tensor_tensor(out=ap(out), in0=ap(a), in1=ap(b), op=op), [out], [a, b])
+
+    def ts(out, a, s1, op0, s2=None, op1=None):
+        if op1 is None:
+            emit("v", lambda: g.vector.tensor_scalar(out=ap(out), in0=ap(a), scalar1=ap(s1), scalar2=None, op0=op0), [out], [a, s1])
+        else:
+            emit("v", lambda: g.vector.tensor_scalar(out=ap(out), in0=ap(a), scalar1=ap(s1), scalar2=ap(s2), op0=op0, op1=op1),
+                 [out], [a, s1, s2])
+
+    def scan(out, d0, d1, op0, op1):
+        emit("v", lambda: g.vector.tensor_tensor_scan(out=ap(out), data0=ap(d0), data1=ap(d1), initial=0.0, op0=op0, op1=op1),
+             [out], [d0, d1])
+
+    def fill(out, c):
+        emit("v", lambda: g.vector.memset(ap(out), c), [out], [])
+
+    def act(out, in_, func=Fn.Copy, bias=0.0, scale=1.0, accum=None):
+        if accum is None:
+            emit("s", lambda: g.scalar.activation(out=ap(out), in_=ap(in_), func=func, bias=ap(bias), scale=ap(scale)),
+                 [out], [in_, bias, scale])
+        else:
+            emit("s", lambda: g.scalar.activation(out=ap(out), in_=ap(in_), func=func, bias=ap(bias), scale=scale,
+                                                  accum_out=ap(accum)), [out, accum], [in_, bias])
+
+    def mm(out, w, x, start, stop):
+        emit("t", lambda: g.tensor.matmul(out=ap(out), lhsT=ap(w), rhs=ap(x), start=start, stop=stop), [out], [w, x])
+
+    def iota(out, pattern, base, mul, flag=False):
+        if flag:
+            emit("g", lambda: g.iota(ap(out), pattern, base, mul, allow_small_or_imprecise_dtypes=True), [out], [])
+        else:
+            emit("g", lambda: g.iota(ap(out), pattern, base, mul), [out], [])
+
+    def dma(q, out, in_, sem, reads, writes):
+        wait_for(q, deps("dma", reads, writes))
+        Q[q].dma_start(out=out, in_=in_).then_inc(T.sem[sem], 16)
+        totals[sem] = totals.get(sem, 0) + 16
+        note("dma", reads, writes, sem, totals[sem], dict(known[q]))
+
+    near = [T.rank_of(d) for d in plan(core, T, topo)[0]]
+    order = [r] + near + [q for q in range(N) if q != r and q not in near]
+    first, last = order[:1 + len(near)], order[1 + len(near):]
+
+    def send(b, grp):
+        wait_for("g", deps("g", [(buf, BL * b, BL * (b + 1)) for buf, s in grp], []))
+        for call in legs(core, T, topo, len(grp)):
+            tr = []
+            for d, j, eng in call:
+                rid, pid = topo.addr(d, core)
+                piece = T[grp[j][0]][:, BL * b:BL * (b + 1)]
+                tr.append(RemoteDMATransfer(dst_ids=[DstId(rid=rid, pnc=pid)], dma_engine_mask=bits(eng),
+                                            remote_sem=T.sem["%s%d" % (grp[j][1], b)], srcs=[piece], dsts=[piece]))
+                totals["loc"] = totals.get("loc", 0) + len(eng)
+            g.remote_dma_fused(tr, local_sem=T.sem.loc)
+
+    for t in range(ROUNDS):
+        for q, src in enumerate(T.cores):
+            for grp in groups(t):
+                got = [(j, eng) for call in legs(src, T, topo, len(grp)) for d, j, eng in call if d == core]
+                got += [y for x, d in plan(src, T, topo)[1] if d == core for y in onward(x, core, topo, len(grp))]
+                for j, eng in got:
+                    buf, s = grp[j]
+                    b = 4 * t + q
+                    note("net", [], [(buf, BL * b, BL * (b + 1))], "%s%d" % (s, b), len(eng), {})
+                    totals["%s%d" % (s, b)] = len(eng)
+
+    c0s = [(8 * t + 2 * r) % 16 for t in range(2)]
+
+    def classes(n, st):
+        return [(n, c0s[st] + m, 16 * (H - 1) + c0s[st] + m + 1, 16) for m in range(2)]
+
+    def consts_v():
+        fill(("o16", 0, 128), -0.0625)
+        fill(("c32c", 0, 1), float(CAP))
+        ts(("cki", 0, 512), ("col", 0, 512), 15, Op.bitwise_and)
+        ts(("dg", 0, 256), ("cki", 0, 256), ("p15", 0, 1), Op.is_equal)
+        for lo, hi in ((0, 512), (512, 1024)):
+            ts(("seg", lo, hi), ("cki", 0, 512), 0.0, Op.is_gt)
+        fill(("neg1", 0, 1), -1.0)
+        fill(("half", 0, 1), 0.5)
+        fill(("mbig", 0, 1), -3.0e7)
+
+    def consts_v2():
+        for t in range(1, ROUNDS):
+            fill(("ln", BL * (4 * t + r), BL * (4 * t + r) + 4), 0.0)
+        for n in ("e1", "ns1"):
+            fill((n, L, LX), 0.0)
+        for i in range(2):
+            fill(("lv%d" % i, L, LX), float(V))
+        fill(("qf0", L, LX), float(V))
+        ts(("kp", 0, 512), ("cki", 0, 512), -512.0, Op.mult, 7680.0, Op.add)
+        ts(("c32", 0, 64), ("col", 0, 64), 31, Op.bitwise_and)
+        ts(("seg32", 0, 64), ("c32", 0, 64), 0.0, Op.is_gt)
+        for c in range(2):
+            ts(("dmp", c, c + 1), ("sc", c, c + 1), 576.0, Op.add)
+            ts(("tri", 32 * c, 32 * c + 32), ("col", 0, 32), ("sc", c, c + 1), Op.is_lt, ("dmp", c, c + 1), Op.mult)
+
+    def consts_g():
+        iota(("en", 0, G0), [[0, G0]], 0, 0, True)
+        iota(("rs", 0, G0), [[0, G0]], -SHIFT - 16384, 0, True)
+        iota(("idc", 0, 512), [[BL, 16], [1, 32]], 4 - SHIFT, 0, True)
+        iota(("jwf", 0, 32), [[BL, 16], [16, 2]], 4, 0, True)
+        iota(("w", 0, IDW), [[1, IDW]], -SHIFT, 0, True)
+        iota(("vn", 0, G0), [[-1, G0]], V, 0, True)
+        iota(("jt", 0, VT), [[1, VT]], 0, 0, True)
+        iota(("vid", 0, IDW), [[0, IDW]], 0, 0, True)
+
+    def names_again(st, lo, hi):
+        act(("qr%d" % st, 16 * lo, 16 * hi), ("I", ("qf%d" % st, 0, LX), ("lrep", lo, hi)), Fn.Identity, ("c1280", 0, 1), -1.0)
+
+    def consts_s():
+        names_again(1, H, L)
+        act(("i1280", 0, 128), ("idn", 0, 128), Fn.Copy, 0.0, 1280.0)
+        act(("bd8", 0, 128), ("bd", 0, 128), Fn.Copy, 0.0, 8192.0)
+        act(("kb", 0, 512), ("seg", 0, 512), Fn.Identity, ("mbig", 0, 1), 6.0e7)
+        for k in range(16):
+            act(("dk", 128 * k, 128 * k + 128), ("idn", 0, 128), Fn.Copy, 0.0, ("dg", k, k + 1))
+        act(("idead", 0, 128), ("idn", 0, 128), Fn.Copy, 0.0, -32768.0)
+        act(("ipen", 0, 128), ("idn", 0, 128), Fn.Copy, 0.0, -64.0)
+
+    def sums(buf, lo, hi):
+        for k in range(16):
+            mm(("bdeg", lo, hi), ("idn", 0, 128), (buf, 16 * lo + k, 16 * (hi - 1) + k + 1, 16), k == 0, k == 15)
+
+    def hits(t):
+        st = t % 2
+        if t == 0:
+            ts(("ok", 0, L), ("bdeg", 0, L), ("limf", 0, 1), Op.is_le)
+        else:
+            tt(("ok", 0, L), ("bdeg", 0, L), ("lmx", 0, L), Op.is_le)
+        if t >= 2:
+            mm(("bhit", 0, L), ("ipen", 0, 128), ("dead%d" % st, 0, L), True, False)
+        mm(("bhit", 0, L), ("bd", 0, 128), ("ok", 0, L), t < 2, True)
+        ts(("hit", 0, L), ("bhit", 0, L), 9.0, Op.is_ge)
+        scan(("cum", 0, LX), ("hit", 0, LX), ("c255", 0, LX), Op.add, Op.min)
+        for c in range(2):
+            act(("sg", c * LX, (c + 1) * LX), ("cum", 0, LX), Fn.Sign, ("sh", c, c + 1), -1.0, ("pla", c, c + 1))
+        if t == 0:
+            ts(("deg", 0, L), ("bdeg", 0, L), -1.0, Op.mult, ("limf", 0, 1), Op.add)
+        else:
+            tt(("deg", 0, L), ("lmx", 0, L), ("bdeg", 0, L), Op.subtract)
+        ts(("plw", 0, 2), ("pla", 0, 2), 0.5, Op.mult, float(LX // 2), Op.add)
+
+    def variables(t, bufs):
+        st, b = t % 2, 4 * t + r
+        ts(("vx", 0, 2), ("pla", 0, 2), 8.0, Op.mult, 8.0 * LX + c0s[st], Op.add)
+        ts(("vy", 0, 2), ("pla", 0, 2), float(2 * H - LX), Op.is_ge, float(1 - V), Op.mult)
+        for buf in bufs:
+            tt((buf, BL * b, BL * b + 2), ("vx", 0, 2), ("vy", 0, 2), Op.add)
+
+    def sizes(t):
+        b = 4 * t + r
+        ts(("la", BL * b + 4, BL * (b + 1)), ("I", ("deg", 0, LX), ("plw", 0, 2)), ("limb", 0, 1), Op.subtract, -256.0, Op.max)
+
+    def dead_of(t):
+        ts(("piv", 0, L), ("cum", 0, L), float(CAP), Op.is_le)
+        tt(("dead%d" % t, 0, L), ("piv", 0, L), ("hit", 0, L), Op.mult)
+
+    def limits(t):
+        act(("a1", 0, 1), ("cum", L - 1, L), Fn.Relu, ("c32c", 0, 1), -1.0)
+        mm(("bhit", 0, 1), ("o16", 0, 128), ("a1", 0, 1), True, True)
+        tc(("ai", 0, 1), ("bhit", 0, 1))
+        ts(("aj", 0, 1), ("ai", 0, 1), 7, Op.bitwise_and)
+        tt(("lima", 0, 1), ("limf", 0, 1), ("aj", 0, 1), Op.add)
+        ts(("limb", 0, 1), ("lima", 0, 1), 1.0, Op.add)
+
+    def list_v(b, buf="la"):
+        tc(("evu", 2 * b, 2 * b + 2), (buf, BL * b, BL * b + 2))
+
+    def list_c(b):
+        tc(("cwu", 2 * b, 2 * b + 2), ("la", BL * b + 2, BL * b + 4))
+
+    def put(table, lo, hi, src):
+        tc(("I", (table, 0, VT), ("evu", 2 * lo, 2 * hi)), src)
+
+    def put_names(b):
+        o, i = ("I", ("nm", 0, VT), ("evu", 2 * b, 2 * b + 2)), ("ln", BL * b + 4, BL * (b + 1))
+        ts(o, i, -1.0, Op.mult, float(V), Op.add)
+
+    def size_of(b):
+        i = 32 * (b % 4)
+        act(("xt", i, i + 32), ("la", BL * b + 4, BL * (b + 1)), Fn.Identity, ("neg1", 0, 1), -1.0)
+
+    def outputs(t):
+        for q in range(N):
+            b = 4 * t + q
+            i = 32 * q
+            size_of(b)
+            act(("nt", i, i + 32), ("ln", BL * b + 4, BL * (b + 1)), Fn.Identity, ("c1280", 0, 1), -1.0)
+            act(("vid", BL * b + 4, BL * (b + 1)), ("I", ("jt", 0, VT), ("evu", 2 * b, 2 * b + 2)))
+        put("nm", 4 * t, 4 * t + 4, ("nt", 0, 128))
+        put("xo", 4 * t, 4 * t + 4, ("xt", 0, 128))
+
+    def picks(t):
+        st = t % 2
+        for lo, hi in CH:
+            act(("xg", 16 * lo, 16 * hi), ("I", ("xm", 0, G0), ("qu%d" % st, lo, hi)))
+
+    def self_picks():
+        for k in range(16):
+            mm(("bself", 0, L), ("dk", 128 * k, 128 * k + 128), ("xg", k, 16 * (L - 1) + k + 1, 16), k == 0, k == 15)
+
+    def main(t):
+        st = t % 2
+
+        def cover(c):
+            lo, hi = CH[c]
+            tt(("eq", 16 * lo, 16 * hi), ("I", ("en", 0, G0), ("qu%d" % st, lo, hi)), ("qr%d" % st, 16 * lo, 16 * hi), Op.is_equal)
+            if t >= 2:
+                mm((PSUM[c], 0, hi - lo), ("idead", 0, 128), ("dead%d" % st, lo, hi), True, False)
+            for k in range(16):
+                mm((PSUM[c], 0, hi - lo), ("i1280", 0, 128), ("eq", 16 * lo + k, 16 * (hi - 1) + k + 1, 16), t < 2 and k == 0, k == 15)
+
+        def uncovered(c):
+            lo, hi = CH[c]
+            tt(("q2", lo, hi), ("qf%d" % st, lo, hi), (PSUM[c], 0, hi - lo), Op.max)
+            ts(("qn", lo, hi), ("q2", lo, hi), float(V), Op.min)
+
+        def pick(c, on):
+            lo, hi = CH[c]
+            o, i = ("xv", 16 * lo, 16 * hi), ("I", ("xm", 0, G0), ("qn", lo, hi))
+            if on == "s":
+                act(o, i, Fn.Relu)
+            else:
+                ts(o, i, 0.0, Op.max)
+
+        def largest(c):
+            lo, hi = CH[c]
+            scan(("msc", 16 * lo, 16 * hi), ("seg", 0, 16 * (hi - lo)), ("xg", 16 * lo, 16 * hi), Op.mult, Op.min)
+
+        cover(0)
+        cover(1)
+        uncovered(0)
+        pick(0, "s")
+        cover(2)
+        uncovered(1)
+        pick(1, "s")
+        sums("xv", *CH[0])
+        largest(0)
+        uncovered(2)
+        pick(2, "v")
+        largest(1)
+        largest(2)
+        ts(("lmx", 0, L), ("msc", 15, 16 * L, 16), ("limb", 0, 1), Op.add, ("lima", 0, 1), Op.min)
+        old = 4 * (t - 1)
+        put("rs", old, old + 4, ("idc", 32 * old, 32 * old + 128))
+        if t > 1:
+            put("rs", 0, old, ("jr", 0, 32 * old))
+        sums("xv", *CH[2])
+        sums("xv", *CH[1])
+
+    def pivots(t):
+        st, b = t % 2, 4 * t + r
+
+        def gathers_claims():
+            act(("xgp", 0, 512), ("I", ("xm", 0, G0), ("qp", 0, 32)), Fn.Relu, ("neg1", 0, 1), -1.0)
+            tc(("slg", 0, 512), ("I", ("rs", 0, G0), ("qp", 0, 32)))
+            mm(("bkey", 0, 512), ("bd8", 0, 128), ("xgp", 0, 512), False, True)
+
+        def own_gathers():
+            self_picks()
+            act(("esg", 0, L), ("bself", 0, L), Fn.Sign, ("half", 0, 1))
+            act(("e1", 0, L), ("esg", 0, L), Fn.Relu, 0.0, float(V))
+            act(("ocx", 0, L), ("q2", 0, L), Fn.Identity, ("c1280", 0, 1), -1.0)
+            act(("e1p", 0, 32), ("I", ("e1", 0, LX), ("plw", 0, 2)))
+
+        def names():
+            tt(("b0", 0, 512), ("xn", 0, 512), ("vr", 0, 512), Op.not_equal)
+            tt(("cc", 0, 512), ("xn", 0, 512), ("b0", 0, 512), Op.mult)
+            scan(("nsc", 0, 512), ("seg", 0, 512), ("cc", 0, 512), Op.mult, Op.max)
+            tt(("ocp", 0, 32), ("I", ("ocx", 0, LX), ("plw", 0, 2)), ("e1p", 0, 32), Op.min)
+            tt(("ocq", 0, 32), ("I", ("ns%d" % st, 0, LX), ("plw", 0, 2)), ("ocp", 0, 32), Op.mult)
+            tt(("ln", BL * b + 4, BL * (b + 1)), ("ocq", 0, 32), ("nsc", 15, 512, 16), Op.max)
+            send(b, [("ln", "n")])
+
+        def claims():
+            tt(("key", 0, 512), ("slg", 0, 512), ("bkey", 0, 512), Op.add)
+            scan(("ksc", 0, 512), ("kb", 0, 512), ("key", 0, 512), Op.min, Op.max)
+            tc(("mi", 0, 32), ("ksc", 15, 512, 16))
+            ts(("mj", 0, 32), ("mi", 0, 32), 511, Op.bitwise_and)
+            tt(("kd", 0, 32), ("mj", 0, 32), ("dg", 0, 32), Op.mult)
+            scan(("kw", 0, 32), ("seg", 0, 32), ("kd", 0, 32), Op.mult, Op.add)
+            for c in range(2):
+                ts(("ke", 32 * c, 32 * c + 32), ("mj", 0, 32), ("kw", 16 * c + 15, 16 * c + 16), Op.is_equal)
+            tt(("kf", 0, 64), ("ke", 0, 64), ("tri", 0, 64), Op.mult)
+            scan(("kg", 0, 64), ("seg32", 0, 64), ("kf", 0, 64), Op.mult, Op.max)
+            tt(("la", BL * b + 2, BL * b + 4), ("kw", 15, 32, 16), ("kg", 31, 64, 32), Op.max)
+            send(b, [("la", "a")])
+
+        tc(("qp", 0, 32), ("I", ("qf%d" % st, 0, LX), ("plw", 0, 2)))
+        mm(("bkey", 0, 512), ("idn", 0, 128), ("kp", 0, 512), True, False)
+        if t < ROUNDS - 1:
+            gathers_claims()
+            tc(("vp", 0, 32), ("I", ("lv%d" % st, 0, LX), ("plw", 0, 2)))
+            act(("xn", 0, 512), ("I", ("en", 0, G0), ("qp", 0, 32)))
+            act(("vr", 0, 512), ("I", ("vn", 0, G0), ("vp", 0, 32)))
+            own_gathers()
+            sizes(t)
+            variables(t, ["la"])
+            if t < 2:
+                dead_of(t)
+            claims()
+            names()
+        else:
+            act(("xn", 0, 512), ("I", ("en", 0, G0), ("qp", 0, 32)))
+            tc(("vp", 0, 32), ("I", ("lv%d" % st, 0, LX), ("plw", 0, 2)))
+            tc(("vr", 0, 512), ("I", ("vn", 0, G0), ("vp", 0, 32)))
+            own_gathers()
+            variables(t, ["ln", "la"])
+            names()
+            gathers_claims()
+            sizes(t)
+            claims()
+
+    def kept_rows(t):
+        st = t % 2
+        tt(("b1", 0, L), ("qf%d" % st, 0, L), ("e1", 0, L), Op.max)
+        if t == 1:
+            tt(("qf1", 0, L), ("q2", 0, L), ("b1", 0, L), Op.min)
+            tc(("qu1", 0, L), ("qf1", 0, L))
+        else:
+            tt(("q3", 0, L), ("q2", 0, L), ("b1", 0, L), Op.min)
+            for m, x in enumerate(classes("nm", st)):
+                act(x, ("q3", m * H, (m + 1) * H))
+
+    def update(t):
+        jo, jn = (None, "jwa", "jwb")[t], (None, "jwb", "jwc")[t]
+        old = 4 * t
+        n = 32 * old
+
+        def land(qs, lists, sz, nms):
+            for q in qs:
+                b = 4 * t + q
+                if lists:
+                    if t > 0:
+                        list_c(b)
+                    list_v(b)
+                if sz:
+                    put("xm", b, b + 1, ("la", BL * b + 4, BL * (b + 1)))
+                if nms:
+                    put("en", b, b + 1, ("ln", BL * b + 4, BL * (b + 1)))
+
+        land(first, True, True, False)
+        land(first, False, False, True)
+        land(last, True, t == 0, False)
+        if t > 0:
+            for q in (3, 2, 1, 0):
+                b = 4 * t + q
+                tc(("I", ("w", 0, IDW), ("cwu", 2 * b, 2 * b + 2)), ("idc", 32 * b, 32 * b + 32))
+            tt(("jd", 0, n), ("I", ("w", 0, IDW), (jo, 0, 2 * old)), ("dg", 0, n), Op.mult)
+            act(("jr", 0, n), ("I", ("w", 0, IDW), (jo, 0, 2 * old)))
+            scan(("js", 0, n), ("seg", 0, n), ("jd", 0, n), Op.mult, Op.add)
+            ts((jn, 0, 2 * old), ("js", 15, n, 16), float(SHIFT), Op.add)
+            act(("xr", 0, n), ("I", ("la", 0, BL * (old + 4)), (jn, 0, 2 * old)))
+            land(last, False, True, False)
+            put("xm", 0, old, ("xr", 0, n))
+        picks(t + 1)
+        land(last, False, False, True)
+        if t > 0:
+            tc(("er", 0, n), ("I", ("ln", 0, BL * (old + 4)), (jn, 0, 2 * old)))
+            put("en", 0, old, ("er", 0, n))
+
+    dma("y", T["nm"][:, 0:V], T.nb[:, :], "dn", [], [("nm", 0, V)])
+    dma("s", T["xm"][:, 0:V], T.xs[:, :], "dx", [], [("xm", 0, V)])
+    dma("s", T["limi"][:, 0:1], T.lim[:, 0:1], "dl", [], [("limi", 0, 1)])
+    dma("y", T["xo"][:, 0:V], T.xs[:, :], "do", [], [("xo", 0, V)])
+    iota(("pii", 0, 1), [[1, 1]], 0, 1)
+    iota(("col", 0, 512), [[1, 512]], 0, 0)
+    fill(("one", 0, 128), 1.0)
+    emit("g", lambda: g.affine_select(T["idn"][:, :], T["one"][:, :], [[-1, 128]], Op.is_equal, 0.0, 0, 1),
+         [("idn", 0, 128)], [("one", 0, 128)])
+    for i in range(2):
+        iota(("lv%d" % i, 0, L), [[1, 2], [16, H]], c0s[i], 0, True)
+    fill(("xm", V, V + 16), 0.0)
+    fill(("hit", L, LX), 1.0)
+    fill(("c255", 0, LX), 255.0)
+    for n in ("deg", "ocx", "ns0"):
+        fill((n, L, LX), 0.0)
+    fill(("qf1", L, LX), float(V))
+    fill(("c1280", 0, 1), float(V))
+    ts(("pij", 0, 1), ("pii", 0, 1), 15, Op.bitwise_and)
+    ts(("pij", 1, 2), ("pii", 0, 1), 4, Op.arith_shift_right)
+    tc(("p15", 0, 1), ("pij", 0, 1))
+    tc(("pg", 0, 1), ("pij", 1, 2))
+    for c in range(2):
+        ts(("sc", c, c + 1), ("p15", 0, 1), 16.0 * c, Op.add)
+        ts(("sh", c, c + 1), ("p15", 0, 1), 16.0 * c + 0.5, Op.add)
+    ts(("gi", 0, 128), ("col", 0, 128), 4, Op.arith_shift_right)
+    ts(("bd", 0, 128), ("gi", 0, 128), ("pg", 0, 1), Op.is_equal)
+    for buf in ("la", "ln"):
+        fill((buf, BL * r, BL * r + 4), 0.0)
+    tc(("lrep", 0, L), ("col", 0, L))
+    tc(("limf", 0, 1), ("limi", 0, 1))
+    ts(("limb", 0, 1), ("limf", 0, 1), 1.0, Op.add)
+
+    for m, x in enumerate(classes("nm", 0)):
+        tc(("qu0", m * H, (m + 1) * H), x)
+    for lo, hi in CH0:
+        mid = (lo + hi) // 2
+        for f, a, z in ((tc, lo, mid), (act, mid, hi)):
+            f(("xv", 16 * a, 16 * z), ("I", ("xm", 0, G0), ("qu0", a, z)))
+        sums("xv", lo, hi)
+    for st in (1, 0):
+        for m, x in enumerate(classes("nm", st)):
+            tc(("qf%d" % st, m * H, (m + 1) * H), x)
+    act(("ocx", 0, L), ("qf0", 0, L), Fn.Identity, ("c1280", 0, 1), -1.0)
+    names_again(1, 0, H)
+    tc(("qu1", 0, L), ("qf1", 0, L))
+    tt(("ns0", 0, L), ("qf0", 0, L), ("lv0", 0, L), Op.not_equal)
+    hits(0)
+    sizes(0)
+    variables(0, ["la"])
+    act(("ocp", 0, 32), ("I", ("ocx", 0, LX), ("plw", 0, 2)))
+    tt(("ln", BL * r + 4, BL * (r + 1)), ("I", ("ns0", 0, LX), ("plw", 0, 2)), ("ocp", 0, 32), Op.mult)
+    send(r, [("la", "a"), ("ln", "n")])
+    consts_g()
+    consts_v()
+    limits(0)
+    consts_s()
+    dead_of(0)
+    tt(("ns1", 0, L), ("qf1", 0, L), ("lv1", 0, L), Op.not_equal)
+    consts_v2()
+    update(0)
+
+    for t in range(1, ROUNDS):
+        main(t)
+        hits(t)
+        pivots(t)
+        if t == 1:
+            for n in ("jwa", "jwb", "jwc"):
+                ts((n, 0, 32), ("jwf", 0, 32), ("p15", 0, 1), Op.add)
+        if t < ROUNDS - 1:
+            limits(t)
+        outputs(t - 1)
+        if t == 1:
+            for lo, hi in CH:
+                names_again(0, lo, hi)
+        kept_rows(t)
+        if t > 1:
+            put_names(4 * (t - 2) + r)
+        if t < ROUNDS - 1:
+            update(t)
+
+    t, old = 3, 12
+    for q in order:
+        b = 4 * t + q
+        list_v(b, "ln")
+        put_names(b)
+    dma("y", T.yn[:, :], T["nm"][:, 0:V], "on", [("nm", 0, V)], [])
+    for q in range(N):
+        b = 4 * t + q
+        act(("vb", 32 * q, 32 * q + 32), ("I", ("jt", 0, VT), ("evu", 2 * b, 2 * b + 2)))
+    for q in order:
+        size_of(4 * t + q)
+        list_c(4 * t + q)
+    put("xo", 12, 16, ("xt", 0, 128))
+    dma("s", T.yx[:, :], T["xo"][:, 0:V], "ox", [("xo", 0, V)], [])
+    for q in (3, 2, 1, 0):
+        b = 4 * t + q
+        tc(("I", ("vid", 0, IDW), ("cwu", 2 * b, 2 * b + 2)), ("vb", 32 * q, 32 * q + 32))
+    tc(("jf", 0, 384), ("I", ("vid", 0, IDW), ("jwc", 0, 24)))
+    put("jt", 0, 8, ("jf", 0, 256))
+    put("jt", 8, old, ("jf", 256, 384))
+    dma("y", T.yj[:, :], T["jt"][0:128:16, 0:V], "oj", [("jt", 0, V)], [])
+    for s, v in totals.items():
+        if known["g"].get(s, 0) < v:
+            g.wait_ge(T.sem[s], v)

@@ -16,31 +16,32 @@ CH = [(0, 64), (64, 128), (128, 160)]
 
 _S = {
     "nm": (VT, FP), "en": (VT, FP), "rs": (VT, FP), "vn": (G0, FP), "jt": (VT, FP), "xm": (VT, BF), "xo": (VT, BF),
-    "la": (576, FP), "ln": (576, FP), "w": (IDW, FP), "vid": (IDW, FP), "vb": (128, FP), "idc": (512, FP),
-    "jwa": (32, U16), "jwb": (32, U16), "jwc": (32, U16), "evu": (32, U16), "cwu": (32, U16), "jwf": (32, FP),
+    "la": (576, FP), "ln": (576, FP), "ksl": (576, FP), "ksn": (128, FP), "w": (IDW, FP), "vid": (IDW, FP), "vb": (128, FP),
+    "idc": (512, FP), "jwa": (32, U16), "jwb": (32, U16), "jwc": (32, U16), "evu": (32, U16), "vc": (64, U16), "cwu": (32, U16),
+    "jwf": (32, FP),
     "qf0": (LX, FP), "qf1": (LX, FP), "qu0": (L, U16), "qu1": (L, U16), "qr0": (16 * L, FP), "qr1": (16 * L, FP),
     "lv0": (LX, FP), "lv1": (LX, FP), "ns0": (LX, FP), "ns1": (LX, FP), "dead0": (L, BF), "dead1": (L, BF),
     "xg": (16 * L, BF), "eq": (16 * L, BF), "xv": (16 * L, BF), "msc": (16 * L, BF), "lmx": (L, FP), "deg": (LX, FP),
     "ocx": (LX, FP), "e1": (LX, FP), "esg": (L, FP), "q2": (L, FP), "q3": (L, FP), "qn": (L, U16), "ok": (L, BF), "hit": (LX, BF),
     "cum": (LX, BF), "c255": (LX, BF), "sg": (2 * LX, BF), "pla": (2, FP), "plw": (2, U16), "vx": (2, FP), "vy": (2, FP),
     "piv": (L, BF),
-    "qp": (32, U16), "vp": (32, U16), "e1p": (32, FP), "ocp": (32, FP), "ocq": (32, FP), "xgp": (512, BF), "slg": (512, FP),
+    "qp": (32, U16), "vp": (32, U16), "e1p": (32, FP), "ocp": (32, FP), "ocq": (32, FP),
     "xn": (512, FP), "vr": (512, FP), "cc": (512, FP), "nsc": (512, FP), "key": (512, FP), "ksc": (512, FP),
     "mi": (32, I32), "mj": (32, I32), "kd": (32, FP),
     "kw": (32, FP), "ke": (64, FP), "kf": (64, FP), "kg": (64, FP), "jd": (256, FP), "js": (256, FP), "jr": (256, FP), "xr": (256, FP),
-    "er": (256, FP), "jf": (384, FP), "xt": (128, FP), "nt": (128, FP), "a1": (1, BF), "ai": (1, I32), "aj": (1, I32),
-    "limi": (1, I32), "limf": (1, FP), "lima": (1, FP), "limb": (1, FP), "c32c": (1, FP), "c1280": (1, FP), "mbig": (1, FP),
-    "neg1": (1, FP), "half": (1, FP),
+    "er": (256, FP), "jf": (384, FP), "xt": (128, BF), "nt": (128, FP), "a1": (1, BF), "ai": (1, I32), "aj": (1, I32),
+    "limi": (1, I32), "limf": (1, FP), "lima": (1, FP), "limb": (1, FP), "kon": (16, FP),
     "one": (128, BF), "idn": (128, BF), "i1280": (128, BF), "idead": (128, BF), "ipen": (128, BF), "bd": (128, BF), "bd8": (128, BF),
-    "dk": (2048, BF), "o16": (128, BF), "pii": (1, I32), "pij": (2, I32), "p15": (1, FP), "pg": (1, FP), "sh": (2, FP), "sc": (2, FP),
+    "dk": (2048, BF), "o16": (128, BF), "pii": (1, I32), "pij": (2, I32), "sh": (2, FP), "sc": (2, FP),
     "dmp": (2, FP), "col": (512, I32), "cki": (512, I32), "gi": (128, I32), "dg": (256, FP), "seg": (1024, BF),
-    "c32": (64, I32), "seg32": (64, BF), "kb": (512, FP), "kp": (512, BF), "tri": (64, FP), "lrep": (L, U16),
+    "c32": (64, I32), "seg32": (64, BF), "kb": (512, FP), "kp": (512, FP), "tri": (64, FP), "lrep": (L, U16),
 }
 PSUM = ["b0", "b1", "b2", "bdeg", "bhit", "bkey", "bself"]
 SCRATCH = {n: ("sbuf", [128, c], d) for n, (c, d) in _S.items()}
 SCRATCH.update({n: ("psum", [128, 512], FP) for n in PSUM})
 SEMAPHORES = (["qv", "qs", "qt", "qg", "dn", "dx", "do", "dl", "on", "ox", "oj", "loc"]
               + ["a%d" % b for b in range(16)] + ["n%d" % b for b in range(16)])
+KON = {n: i for i, n in enumerate(["neg1", "half", "c33", "kv0", "kv1", "c32c", "c1280", "mbig", "p15", "pg"])}
 
 
 def plan(core, T, topo):
@@ -60,7 +61,7 @@ def bits(engines):
 
 def groups(t):
     a, n = ("la", "a"), ("ln", "n")
-    return [[a, n]] if t == 0 else [[a], [n]] if t < ROUNDS - 1 else [[n], [a]]
+    return [[a, n]] if t == 0 else [[a], [n]]
 
 
 def share(engines, n, i):
@@ -158,11 +159,15 @@ def rank_program(g, core, T, topo):
             h[:] = [e for e in h if not (e[2] == "r" and e[3] == q and q in cnt and lo <= e[0] and e[1] <= hi)]
             h.append((lo, hi, "r", q, sem, val, snap))
 
+    def real(x):
+        return ("kon", KON[x[0]], KON[x[0]] + 1) if x[0] in KON else x
+
     def flat(x):
         if not isinstance(x, tuple):
             return []
         if x[0] == "I":
             return flat(x[1]) + flat(x[2])
+        x = real(x)
         return [(x[0], x[1], x[2])]
 
     def ap(x):
@@ -170,6 +175,7 @@ def rank_program(g, core, T, topo):
             return x
         if x[0] == "I":
             return ap(x[1]).indirect(ap(x[2]))
+        x = real(x)
         if len(x) > 3:
             return T[x[0]][:, x[1]:x[2]:x[3]]
         return T[x[0]][:, x[1]:x[2]]
@@ -294,12 +300,14 @@ def rank_program(g, core, T, topo):
         for c in range(2):
             ts(("dmp", c, c + 1), ("sc", c, c + 1), 576.0, Op.add)
             ts(("tri", 32 * c, 32 * c + 32), ("col", 0, 32), ("sc", c, c + 1), Op.is_lt, ("dmp", c, c + 1), Op.mult)
+        for n in ("jwa", "jwb", "jwc"):
+            ts((n, 0, 32), ("jwf", 0, 32), ("p15", 0, 1), Op.add)
 
     def consts_g():
+        iota(("jwf", 0, 32), [[BL, 16], [16, 2]], 4, 0, True)
         iota(("en", 0, G0), [[0, G0]], 0, 0, True)
         iota(("rs", 0, G0), [[0, G0]], -SHIFT - 16384, 0, True)
         iota(("idc", 0, 512), [[BL, 16], [1, 32]], 4 - SHIFT, 0, True)
-        iota(("jwf", 0, 32), [[BL, 16], [16, 2]], 4, 0, True)
         iota(("w", 0, IDW), [[1, IDW]], -SHIFT, 0, True)
         iota(("vn", 0, G0), [[-1, G0]], V, 0, True)
         iota(("jt", 0, VT), [[1, VT]], 0, 0, True)
@@ -323,7 +331,9 @@ def rank_program(g, core, T, topo):
             mm(("bdeg", lo, hi), ("idn", 0, 128), (buf, 16 * lo + k, 16 * (hi - 1) + k + 1, 16), k == 0, k == 15)
 
     def hits(t):
-        st = t % 2
+        st, old = t % 2, 4 * (t - 1)
+        if t > 0:
+            put("rs", old, old + 4, ("ksn", 0, 128))
         if t == 0:
             ts(("ok", 0, L), ("bdeg", 0, L), ("limf", 0, 1), Op.is_le)
         else:
@@ -339,14 +349,16 @@ def rank_program(g, core, T, topo):
             ts(("deg", 0, L), ("bdeg", 0, L), -1.0, Op.mult, ("limf", 0, 1), Op.add)
         else:
             tt(("deg", 0, L), ("lmx", 0, L), ("bdeg", 0, L), Op.subtract)
+        if t > 1:
+            put("rs", 0, old, ("jr", 0, 32 * old))
         ts(("plw", 0, 2), ("pla", 0, 2), 0.5, Op.mult, float(LX // 2), Op.add)
 
-    def variables(t, bufs):
+    def variables(t):
         st, b = t % 2, 4 * t + r
-        ts(("vx", 0, 2), ("pla", 0, 2), 8.0, Op.mult, 8.0 * LX + c0s[st], Op.add)
-        ts(("vy", 0, 2), ("pla", 0, 2), float(2 * H - LX), Op.is_ge, float(1 - V), Op.mult)
-        for buf in bufs:
-            tt((buf, BL * b, BL * b + 2), ("vx", 0, 2), ("vy", 0, 2), Op.add)
+        act(("vy", 0, 2), ("pla", 0, 2), Fn.Sign, ("c33", 0, 1))
+        act(("vx", 0, 2), ("vy", 0, 2), Fn.Identity, ("kv%d" % st, 0, 1), (1 - V) / 2.0)
+        for c in range(2):
+            act(("la", BL * b + c, BL * b + c + 1), ("pla", c, c + 1), Fn.Identity, ("vx", c, c + 1), 8.0)
 
     def sizes(t):
         b = 4 * t + r
@@ -356,16 +368,18 @@ def rank_program(g, core, T, topo):
         ts(("piv", 0, L), ("cum", 0, L), float(CAP), Op.is_le)
         tt(("dead%d" % t, 0, L), ("piv", 0, L), ("hit", 0, L), Op.mult)
 
-    def limits(t):
+    def count(t):
         act(("a1", 0, 1), ("cum", L - 1, L), Fn.Relu, ("c32c", 0, 1), -1.0)
         mm(("bhit", 0, 1), ("o16", 0, 128), ("a1", 0, 1), True, True)
+
+    def limits(t):
         tc(("ai", 0, 1), ("bhit", 0, 1))
         ts(("aj", 0, 1), ("ai", 0, 1), 7, Op.bitwise_and)
         tt(("lima", 0, 1), ("limf", 0, 1), ("aj", 0, 1), Op.add)
         ts(("limb", 0, 1), ("lima", 0, 1), 1.0, Op.add)
 
-    def list_v(b, buf="la"):
-        tc(("evu", 2 * b, 2 * b + 2), (buf, BL * b, BL * b + 2))
+    def list_v(b):
+        tc(("evu", 2 * b, 2 * b + 2), ("la", BL * b, BL * b + 2))
 
     def list_c(b):
         tc(("cwu", 2 * b, 2 * b + 2), ("la", BL * b + 2, BL * b + 4))
@@ -385,7 +399,6 @@ def rank_program(g, core, T, topo):
         for q in range(N):
             b = 4 * t + q
             i = 32 * q
-            size_of(b)
             act(("nt", i, i + 32), ("ln", BL * b + 4, BL * (b + 1)), Fn.Identity, ("c1280", 0, 1), -1.0)
             act(("vid", BL * b + 4, BL * (b + 1)), ("I", ("jt", 0, VT), ("evu", 2 * b, 2 * b + 2)))
         put("nm", 4 * t, 4 * t + 4, ("nt", 0, 128))
@@ -401,7 +414,7 @@ def rank_program(g, core, T, topo):
             mm(("bself", 0, L), ("dk", 128 * k, 128 * k + 128), ("xg", k, 16 * (L - 1) + k + 1, 16), k == 0, k == 15)
 
     def main(t):
-        st = t % 2
+        st, old = t % 2, 4 * (t - 1)
 
         def cover(c):
             lo, hi = CH[c]
@@ -429,6 +442,7 @@ def rank_program(g, core, T, topo):
             scan(("msc", 16 * lo, 16 * hi), ("seg", 0, 16 * (hi - lo)), ("xg", 16 * lo, 16 * hi), Op.mult, Op.min)
 
         cover(0)
+        tt(("ksn", 0, 128), ("idc", 32 * old, 32 * old + 128), ("bkey", 0, 128), Op.add)
         cover(1)
         uncovered(0)
         pick(0, "s")
@@ -442,20 +456,21 @@ def rank_program(g, core, T, topo):
         largest(1)
         largest(2)
         ts(("lmx", 0, L), ("msc", 15, 16 * L, 16), ("limb", 0, 1), Op.add, ("lima", 0, 1), Op.min)
-        old = 4 * (t - 1)
-        put("rs", old, old + 4, ("idc", 32 * old, 32 * old + 128))
+        for q in range(N):
+            act(("ksl", BL * (old + q) + 4, BL * (old + q + 1)), ("ksn", 32 * q, 32 * q + 32))
         if t > 1:
-            put("rs", 0, old, ("jr", 0, 32 * old))
+            act(("jr", 0, 32 * old), ("I", ("ksl", 0, BL * (old + 4)), (("jwb", "jwc")[t - 2], 0, 2 * old)))
+        for c in range(2):
+            tc(("evu", 2 * old + c, 2 * old + 7 + c, 2), ("la", BL * old + c, BL * (old + 3) + c + 1, BL))
         sums("xv", *CH[2])
         sums("xv", *CH[1])
 
     def pivots(t):
         st, b = t % 2, 4 * t + r
 
-        def gathers_claims():
-            act(("xgp", 0, 512), ("I", ("xm", 0, G0), ("qp", 0, 32)), Fn.Relu, ("neg1", 0, 1), -1.0)
-            tc(("slg", 0, 512), ("I", ("rs", 0, G0), ("qp", 0, 32)))
-            mm(("bkey", 0, 512), ("bd8", 0, 128), ("xgp", 0, 512), False, True)
+        def keys():
+            tt(("key", 0, 512), ("I", ("rs", 0, G0), ("qp", 0, 32)), ("kp", 0, 512), Op.add)
+            scan(("ksc", 0, 512), ("kb", 0, 512), ("key", 0, 512), Op.min, Op.max)
 
         def own_gathers():
             self_picks()
@@ -465,7 +480,7 @@ def rank_program(g, core, T, topo):
             act(("e1p", 0, 32), ("I", ("e1", 0, LX), ("plw", 0, 2)))
 
         def names():
-            tt(("b0", 0, 512), ("xn", 0, 512), ("vr", 0, 512), Op.not_equal)
+            tt(("b0", 0, 512), ("xn", 0, 512), ("b1", 0, 512), Op.not_equal)
             tt(("cc", 0, 512), ("xn", 0, 512), ("b0", 0, 512), Op.mult)
             scan(("nsc", 0, 512), ("seg", 0, 512), ("cc", 0, 512), Op.mult, Op.max)
             tt(("ocp", 0, 32), ("I", ("ocx", 0, LX), ("plw", 0, 2)), ("e1p", 0, 32), Op.min)
@@ -474,8 +489,6 @@ def rank_program(g, core, T, topo):
             send(b, [("ln", "n")])
 
         def claims():
-            tt(("key", 0, 512), ("slg", 0, 512), ("bkey", 0, 512), Op.add)
-            scan(("ksc", 0, 512), ("kb", 0, 512), ("key", 0, 512), Op.min, Op.max)
             tc(("mi", 0, 32), ("ksc", 15, 512, 16))
             ts(("mj", 0, 32), ("mi", 0, 32), 511, Op.bitwise_and)
             tt(("kd", 0, 32), ("mj", 0, 32), ("dg", 0, 32), Op.mult)
@@ -488,29 +501,22 @@ def rank_program(g, core, T, topo):
             send(b, [("la", "a")])
 
         tc(("qp", 0, 32), ("I", ("qf%d" % st, 0, LX), ("plw", 0, 2)))
-        mm(("bkey", 0, 512), ("idn", 0, 128), ("kp", 0, 512), True, False)
+        act(("xn", 0, 512), ("I", ("en", 0, G0), ("qp", 0, 32)))
+        keys()
+        tc(("vp", 0, 32), ("I", ("lv%d" % st, 0, LX), ("plw", 0, 2)))
+        variables(t)
         if t < ROUNDS - 1:
-            gathers_claims()
-            tc(("vp", 0, 32), ("I", ("lv%d" % st, 0, LX), ("plw", 0, 2)))
-            act(("xn", 0, 512), ("I", ("en", 0, G0), ("qp", 0, 32)))
-            act(("vr", 0, 512), ("I", ("vn", 0, G0), ("vp", 0, 32)))
-            own_gathers()
-            sizes(t)
-            variables(t, ["la"])
-            if t < 2:
-                dead_of(t)
-            claims()
-            names()
-        else:
-            act(("xn", 0, 512), ("I", ("en", 0, G0), ("qp", 0, 32)))
-            tc(("vp", 0, 32), ("I", ("lv%d" % st, 0, LX), ("plw", 0, 2)))
-            tc(("vr", 0, 512), ("I", ("vn", 0, G0), ("vp", 0, 32)))
-            own_gathers()
-            variables(t, ["ln", "la"])
-            names()
-            gathers_claims()
-            sizes(t)
-            claims()
+            count(t)
+        act(("vr", 0, 512), ("I", ("vn", 0, G0), ("vp", 0, 32)))
+        act(("b1", 0, 512), ("vr", 0, 512))
+        own_gathers()
+        sizes(t)
+        claims()
+        if t < ROUNDS - 1:
+            limits(t)
+        if t < 2:
+            dead_of(t)
+        names()
 
     def kept_rows(t):
         st = t % 2
@@ -528,27 +534,29 @@ def rank_program(g, core, T, topo):
         old = 4 * t
         n = 32 * old
 
+        def place(table, b, src):
+            tc(("I", (table, 0, VT), ("vc", 4 * b, 4 * b + 2)), src)
+
         def land(qs, lists, sz, nms):
             for q in qs:
                 b = 4 * t + q
                 if lists:
-                    if t > 0:
-                        list_c(b)
-                    list_v(b)
+                    tc(("vc", 4 * b, 4 * b + 4), ("la", BL * b, BL * b + 4))
+                    size_of(b)
                 if sz:
-                    put("xm", b, b + 1, ("la", BL * b + 4, BL * (b + 1)))
+                    place("xm", b, ("la", BL * b + 4, BL * (b + 1)))
                 if nms:
-                    put("en", b, b + 1, ("ln", BL * b + 4, BL * (b + 1)))
+                    place("en", b, ("ln", BL * b + 4, BL * (b + 1)))
 
         land(first, True, True, False)
         land(first, False, False, True)
         land(last, True, t == 0, False)
+        mm(("bkey", 0, 128), ("bd8", 0, 128), ("xt", 0, 128), True, True)
         if t > 0:
             for q in (3, 2, 1, 0):
                 b = 4 * t + q
-                tc(("I", ("w", 0, IDW), ("cwu", 2 * b, 2 * b + 2)), ("idc", 32 * b, 32 * b + 32))
+                tc(("I", ("w", 0, IDW), ("vc", 4 * b + 2, 4 * b + 4)), ("idc", 32 * b, 32 * b + 32))
             tt(("jd", 0, n), ("I", ("w", 0, IDW), (jo, 0, 2 * old)), ("dg", 0, n), Op.mult)
-            act(("jr", 0, n), ("I", ("w", 0, IDW), (jo, 0, 2 * old)))
             scan(("js", 0, n), ("seg", 0, n), ("jd", 0, n), Op.mult, Op.add)
             ts((jn, 0, 2 * old), ("js", 15, n, 16), float(SHIFT), Op.add)
             act(("xr", 0, n), ("I", ("la", 0, BL * (old + 4)), (jn, 0, 2 * old)))
@@ -563,6 +571,7 @@ def rank_program(g, core, T, topo):
     dma("y", T["nm"][:, 0:V], T.nb[:, :], "dn", [], [("nm", 0, V)])
     dma("s", T["xm"][:, 0:V], T.xs[:, :], "dx", [], [("xm", 0, V)])
     dma("s", T["limi"][:, 0:1], T.lim[:, 0:1], "dl", [], [("limi", 0, 1)])
+    wait_for("y", [("dn", 16, {})])
     dma("y", T["xo"][:, 0:V], T.xs[:, :], "do", [], [("xo", 0, V)])
     iota(("pii", 0, 1), [[1, 1]], 0, 1)
     iota(("col", 0, 512), [[1, 512]], 0, 0)
@@ -578,6 +587,10 @@ def rank_program(g, core, T, topo):
         fill((n, L, LX), 0.0)
     fill(("qf1", L, LX), float(V))
     fill(("c1280", 0, 1), float(V))
+    fill(("ksl", 0, 576), 0.0)
+    fill(("c33", 0, 1), float(LX - 2 * H + 1))
+    for i in range(2):
+        fill(("kv%d" % i, 0, 1), 8.0 * LX + c0s[i] + (1 - V) / 2.0)
     ts(("pij", 0, 1), ("pii", 0, 1), 15, Op.bitwise_and)
     ts(("pij", 1, 2), ("pii", 0, 1), 4, Op.arith_shift_right)
     tc(("p15", 0, 1), ("pij", 0, 1))
@@ -609,12 +622,13 @@ def rank_program(g, core, T, topo):
     tt(("ns0", 0, L), ("qf0", 0, L), ("lv0", 0, L), Op.not_equal)
     hits(0)
     sizes(0)
-    variables(0, ["la"])
-    act(("ocp", 0, 32), ("I", ("ocx", 0, LX), ("plw", 0, 2)))
+    variables(0)
+    tc(("ocp", 0, 32), ("I", ("ocx", 0, LX), ("plw", 0, 2)))
     tt(("ln", BL * r + 4, BL * (r + 1)), ("I", ("ns0", 0, LX), ("plw", 0, 2)), ("ocp", 0, 32), Op.mult)
     send(r, [("la", "a"), ("ln", "n")])
     consts_g()
     consts_v()
+    count(0)
     limits(0)
     consts_s()
     dead_of(0)
@@ -626,11 +640,6 @@ def rank_program(g, core, T, topo):
         main(t)
         hits(t)
         pivots(t)
-        if t == 1:
-            for n in ("jwa", "jwb", "jwc"):
-                ts((n, 0, 32), ("jwf", 0, 32), ("p15", 0, 1), Op.add)
-        if t < ROUNDS - 1:
-            limits(t)
         outputs(t - 1)
         if t == 1:
             for lo, hi in CH:
@@ -642,23 +651,33 @@ def rank_program(g, core, T, topo):
             update(t)
 
     t, old = 3, 12
-    for q in order:
-        b = 4 * t + q
-        list_v(b, "ln")
-        put_names(b)
-    dma("y", T.yn[:, :], T["nm"][:, 0:V], "on", [("nm", 0, V)], [])
-    for q in range(N):
-        b = 4 * t + q
-        act(("vb", 32 * q, 32 * q + 32), ("I", ("jt", 0, VT), ("evu", 2 * b, 2 * b + 2)))
-    for q in order:
-        size_of(4 * t + q)
-        list_c(4 * t + q)
-    put("xo", 12, 16, ("xt", 0, 128))
-    dma("s", T.yx[:, :], T["xo"][:, 0:V], "ox", [("xo", 0, V)], [])
+
+    def lands(qs):
+        for q in qs:
+            b = 4 * t + q
+            list_v(b)
+            act(("vb", 32 * q, 32 * q + 32), ("I", ("jt", 0, VT), ("evu", 2 * b, 2 * b + 2)))
+            size_of(b)
+            list_c(b)
+
+    def sizes_out(qs):
+        for q in qs:
+            put("xo", 12 + q, 13 + q, ("xt", 32 * q, 32 * q + 32))
+
+    lands(first)
+    sizes_out(first)
+    for q in first:
+        put_names(12 + q)
+    lands(last)
     for q in (3, 2, 1, 0):
-        b = 4 * t + q
-        tc(("I", ("vid", 0, IDW), ("cwu", 2 * b, 2 * b + 2)), ("vb", 32 * q, 32 * q + 32))
-    tc(("jf", 0, 384), ("I", ("vid", 0, IDW), ("jwc", 0, 24)))
+        tc(("I", ("vid", 0, IDW), ("cwu", 24 + 2 * q, 26 + 2 * q)), ("vb", 32 * q, 32 * q + 32))
+    for lo, hi in ((0, 8), (8, old)):
+        act(("jf", 32 * lo, 32 * hi), ("I", ("vid", 0, IDW), ("jwc", 2 * lo, 2 * hi)))
+    sizes_out(last)
+    dma("s", T.yx[:, :], T["xo"][:, 0:V], "ox", [("xo", 0, V)], [])
+    for q in last:
+        put_names(12 + q)
+    dma("y", T.yn[:, :], T["nm"][:, 0:V], "on", [("nm", 0, V)], [])
     put("jt", 0, 8, ("jf", 0, 256))
     put("jt", 8, old, ("jf", 256, 384))
     dma("y", T.yj[:, :], T["jt"][0:128:16, 0:V], "oj", [("jt", 0, V)], [])

from concourse.bass import DstId, RemoteDMATransfer
from concourse.mybir import AluOpType as Op, ActivationFunctionType as Fn

V, H, CAP, ROUNDS = 1280, 80, 32, 4
N = 4
L = 2 * H
LX = L + CAP
VT = 1792
G0 = 1288
BL = 36
IDW = 640
SHIFT = 512 * 32618
FP, BF, I32, U16 = "float32", "bfloat16", "int32", "uint16"
CH0 = [(0, 64), (64, 160)]
CH = [(0, 64), (64, 128), (128, 160)]

_S = {
    "nm": (VT, FP), "en": (VT, FP), "rs": (VT, FP), "vn": (G0, FP), "jt": (VT, FP), "xm": (VT, BF), "xo": (VT, BF),
    "la": (576, FP), "ln": (576, FP), "ksl": (576, FP), "ksn": (128, FP), "w": (IDW, FP), "vid": (IDW, FP), "vb": (128, FP),
    "idc": (512, FP), "jwa": (32, U16), "jwb": (32, U16), "jwc": (32, U16), "evu": (32, U16), "vc": (64, U16), "cwu": (32, U16),
    "jwf": (32, FP),
    "qf0": (LX, FP), "qf1": (LX, FP), "qu0": (L, U16), "qu1": (L, U16), "qr0": (16 * L, FP), "qr1": (16 * L, FP),
    "lv0": (LX, FP), "lv1": (LX, FP), "ns0": (LX, FP), "ns1": (LX, FP), "dead0": (L, BF), "dead1": (L, BF),
    "xg": (16 * L, BF), "eq": (16 * L, BF), "xv": (16 * L, BF), "msc": (16 * L, BF), "lmx": (L, FP), "deg": (LX, FP),
    "ocx": (LX, FP), "e1": (LX, FP), "esg": (L, FP), "q2": (L, FP), "q3": (L, FP), "qn": (L, U16), "ok": (L, BF), "hit": (LX, BF),
    "cum": (LX, BF), "c255": (LX, BF), "sg": (2 * LX, BF), "pla": (2, FP), "plw": (2, U16), "vx": (2, FP), "vy": (2, FP),
    "piv": (L, BF),
    "qp": (32, U16), "vp": (32, U16), "e1p": (32, FP), "ocp": (32, FP), "ocq": (32, FP),
    "xn": (512, FP), "vr": (512, FP), "cc": (512, FP), "nsc": (512, FP), "key": (512, FP), "ksc": (512, FP),
    "mi": (32, I32), "mj": (32, I32), "kd": (32, FP),
    "kw": (32, FP), "ke": (64, FP), "kf": (64, FP), "kg": (64, FP), "jd": (256, FP), "js": (256, FP), "jr": (256, FP), "xr": (256, FP),
    "er": (256, FP), "jf": (384, FP), "xt": (128, BF), "nt": (128, FP), "a1": (1, BF), "ai": (1, I32), "aj": (1, I32),
    "limi": (1, I32), "limf": (1, FP), "lima": (1, FP), "limb": (1, FP), "kon": (16, FP),
    "one": (128, BF), "idn": (128, BF), "i1280": (128, BF), "idead": (128, BF), "ipen": (128, BF), "bd": (128, BF), "bd8": (128, BF),
    "dk": (2048, BF), "o16": (128, BF), "pii": (1, I32), "pij": (2, I32), "sh": (2, FP), "sc": (2, FP),
    "dmp": (2, FP), "col": (512, I32), "cki": (512, I32), "gi": (128, I32), "dg": (256, FP), "seg": (1024, BF),
    "c32": (64, I32), "seg32": (64, BF), "kb": (512, FP), "kp": (512, FP), "tri": (64, FP), "lrep": (L, U16),
}
PSUM = ["b0", "b1", "b2", "bdeg", "bhit", "bkey", "bself"]
SCRATCH = {n: ("sbuf", [128, c], d) for n, (c, d) in _S.items()}
SCRATCH.update({n: ("psum", [128, 512], FP) for n in PSUM})
SEMAPHORES = (["qv", "qs", "qt", "qg", "dn", "dx", "do", "dl", "on", "ox", "oj", "loc"]
              + ["a%d" % b for b in range(16)] + ["n%d" % b for b in range(16)])
KON = {n: i for i, n in enumerate(["neg1", "half", "c33", "kv0", "kv1", "c32c", "c1280", "mbig", "p15", "pg"])}


def plan(core, T, topo):
    direct = [d for d in T.cores if d != core and topo.may_write(core, d)]
    rest = [d for d in T.cores if d != core and not topo.may_write(core, d)]
    relays = []
    for d in rest:
        ok = [x for x in topo.cores_of(core) if x not in T.cores and x not in relays and topo.may_write(x, d)]
        ok.sort(key=lambda x: (topo.die(x) != topo.die(core), x))
        relays.append(ok[0])
    return direct, list(zip(relays, rest))


def bits(engines):
    return sum(1 << e for e in engines)


def groups(t):
    a, n = ("la", "a"), ("ln", "n")
    return [[a, n]] if t == 0 else [[a], [n]]


def share(engines, n, i):
    k = len(engines) // n
    return engines[i * k:(i + 1) * k]


def legs(core, T, topo, m):
    direct, via = plan(core, T, topo)
    relays = [x for x, d in via]
    return [[(d, j, share(topo.engines(core, d), len(ds) * m, i * m + j)) for i, d in enumerate(ds) for j in range(m)]
            for ds in (relays, direct)]


def onward(x, dst, topo, m):
    return [(j, share(topo.engines(x, dst), m, j)) for j in range(m)]


def relay_program(g, core, T, topo):
    for r, src in enumerate(T.cores):
        for x, dst in plan(src, T, topo)[1]:
            if x != core:
                continue
            rid, pid = topo.addr(dst, core)
            n = 0
            for t in range(ROUNDS):
                b = 4 * t + r
                for grp in groups(t):
                    for call in legs(src, T, topo, len(grp)):
                        for d, j, eng in call:
                            if d == core:
                                g.wait_ge(T.sem["%s%d" % (grp[j][1], b)], len(eng))
                    tr = []
                    for j, eng in onward(core, dst, topo, len(grp)):
                        piece = T[grp[j][0]][:, BL * b:BL * (b + 1)]
                        tr.append(RemoteDMATransfer(dst_ids=[DstId(rid=rid, pnc=pid)], dma_engine_mask=bits(eng),
                                                    remote_sem=T.sem["%s%d" % (grp[j][1], b)], srcs=[piece], dsts=[piece]))
                        n += len(eng)
                    g.remote_dma_fused(tr, local_sem=T.sem.loc)
            g.wait_ge(T.sem.loc, n)


def rank_program(g, core, T, topo):
    rank = T.rank_of(core)
    if rank is None:
        relay_program(g, core, T, topo)
        return
    r = rank
    Q = {"v": g.vector, "s": g.scalar, "t": g.tensor, "g": g, "y": g.sync}
    cnt = {q: 0 for q in "vstg"}
    known = {q: {} for q in "vstgy"}
    hist = {}
    totals = {}

    def is_psum(n):
        return n in PSUM

    def deps(q, reads, writes):
        toks = []
        for kind, regs in (("r", reads), ("w", writes)):
            for n, lo, hi in regs:
                for e in hist.get(n, ()):
                    if not is_psum(n) and (e[1] <= lo or hi <= e[0]):
                        continue
                    if kind == "r" and e[2] == "r" and not is_psum(n):
                        continue
                    if is_psum(n) and e[3] == q and (q == "t" or kind == "r" and e[2] == "r"):
                        continue
                    toks.append((e[4], e[5], e[6]))
        return toks

    def wait_for(q, toks):
        need = {}
        k = known[q]
        for s, v, snap in toks:
            if need.get(s, (0, None))[0] < v:
                need[s] = (v, snap)
        for s in list(need):
            v = need[s][0]
            if k.get(s, 0) >= v or any(o != s and sn.get(s, 0) >= v and k.get(o, 0) < ov for o, (ov, sn) in need.items()):
                continue
            Q[q].wait_ge(T.sem[s], v)
        for s, (v, snap) in need.items():
            k[s] = max(k.get(s, 0), v)
            for o, ov in snap.items():
                k[o] = max(k.get(o, 0), ov)

    def note(q, reads, writes, sem, val, snap):
        for n, lo, hi in writes:
            h = hist.setdefault(n, [])
            h[:] = [e for e in h if not (lo <= e[0] and e[1] <= hi)]
            h.append((lo, hi, "w", q, sem, val, snap))
        for n, lo, hi in reads:
            h = hist.setdefault(n, [])
            h[:] = [e for e in h if not (e[2] == "r" and e[3] == q and q in cnt and lo <= e[0] and e[1] <= hi)]
            h.append((lo, hi, "r", q, sem, val, snap))

    def real(x):
        return ("kon", KON[x[0]], KON[x[0]] + 1) if x[0] in KON else x

    def flat(x):
        if not isinstance(x, tuple):
            return []
        if x[0] == "I":
            return flat(x[1]) + flat(x[2])
        x = real(x)
        return [(x[0], x[1], x[2])]

    def ap(x):
        if not isinstance(x, tuple):
            return x
        if x[0] == "I":
            return ap(x[1]).indirect(ap(x[2]))
        x = real(x)
        if len(x) > 3:
            return T[x[0]][:, x[1]:x[2]:x[3]]
        return T[x[0]][:, x[1]:x[2]]

    def emit(q, fn, outs, ins):
        reads, writes = [], []
        for x in ins:
            reads += flat(x)
        for x in outs:
            if isinstance(x, tuple) and x[0] == "I":
                writes += flat(x[1])
                reads += flat(x[2])
            else:
                writes += flat(x)
        wait_for(q, deps(q, reads, writes))
        inst = fn()
        sem = "q" + q
        cnt[q] += 1
        inst.then_inc(T.sem[sem], 1)
        totals[sem] = cnt[q]
        snap = dict(known[q])
        snap[sem] = cnt[q]
        note(q, reads, writes, sem, cnt[q], snap)

    def tc(out, in_):
        emit("v", lambda: g.vector.tensor_copy(out=ap(out), in_=ap(in_)), [out], [in_])

    def tt(out, a, b, op):
        emit("v", lambda: g.vector.tensor_tensor(out=ap(out), in0=ap(a), in1=ap(b), op=op), [out], [a, b])

    def ts(out, a, s1, op0, s2=None, op1=None):
        if op1 is None:
            emit("v", lambda: g.vector.tensor_scalar(out=ap(out), in0=ap(a), scalar1=ap(s1), scalar2=None, op0=op0), [out], [a, s1])
        else:
            emit("v", lambda: g.vector.tensor_scalar(out=ap(out), in0=ap(a), scalar1=ap(s1), scalar2=ap(s2), op0=op0, op1=op1),
                 [out], [a, s1, s2])

    def scan(out, d0, d1, op0, op1):
        emit("v", lambda: g.vector.tensor_tensor_scan(out=ap(out), data0=ap(d0), data1=ap(d1), initial=0.0, op0=op0, op1=op1),
             [out], [d0, d1])

    def fill(out, c):
        emit("v", lambda: g.vector.memset(ap(out), c), [out], [])

    def act(out, in_, func=Fn.Copy, bias=0.0, scale=1.0, accum=None):
        if accum is None:
            emit("s", lambda: g.scalar.activation(out=ap(out), in_=ap(in_), func=func, bias=ap(bias), scale=ap(scale)),
                 [out], [in_, bias, scale])
        else:
            emit("s", lambda: g.scalar.activation(out=ap(out), in_=ap(in_), func=func, bias=ap(bias), scale=scale,
                                                  accum_out=ap(accum)), [out, accum], [in_, bias])

    def mm(out, w, x, start, stop):
        emit("t", lambda: g.tensor.matmul(out=ap(out), lhsT=ap(w), rhs=ap(x), start=start, stop=stop), [out], [w, x])

    def iota(out, pattern, base, mul, flag=False):
        if flag:
            emit("g", lambda: g.iota(ap(out), pattern, base, mul, allow_small_or_imprecise_dtypes=True), [out], [])
        else:
            emit("g", lambda: g.iota(ap(out), pattern, base, mul), [out], [])

    def dma(q, out, in_, sem, reads, writes):
        wait_for(q, deps("dma", reads, writes))
        Q[q].dma_start(out=out, in_=in_).then_inc(T.sem[sem], 16)
        totals[sem] = totals.get(sem, 0) + 16
        note("dma", reads, writes, sem, totals[sem], dict(known[q]))

    near = [T.rank_of(d) for d in plan(core, T, topo)[0]]
    order = [r] + near + [q for q in range(N) if q != r and q not in near]
    first, last = order[:1 + len(near)], order[1 + len(near):]

    def send(b, grp):
        wait_for("g", deps("g", [(buf, BL * b, BL * (b + 1)) for buf, s in grp], []))
        for call in legs(core, T, topo, len(grp)):
            tr = []
            for d, j, eng in call:
                rid, pid = topo.addr(d, core)
                piece = T[grp[j][0]][:, BL * b:BL * (b + 1)]
                tr.append(RemoteDMATransfer(dst_ids=[DstId(rid=rid, pnc=pid)], dma_engine_mask=bits(eng),
                                            remote_sem=T.sem["%s%d" % (grp[j][1], b)], srcs=[piece], dsts=[piece]))
                totals["loc"] = totals.get("loc", 0) + len(eng)
            g.remote_dma_fused(tr, local_sem=T.sem.loc)

    for t in range(ROUNDS):
        for q, src in enumerate(T.cores):
            for grp in groups(t):
                got = [(j, eng) for call in legs(src, T, topo, len(grp)) for d, j, eng in call if d == core]
                got += [y for x, d in plan(src, T, topo)[1] if d == core for y in onward(x, core, topo, len(grp))]
                for j, eng in got:
                    buf, s = grp[j]
                    b = 4 * t + q
                    note("net", [], [(buf, BL * b, BL * (b + 1))], "%s%d" % (s, b), len(eng), {})
                    totals["%s%d" % (s, b)] = len(eng)

    c0s = [(8 * t + 2 * r) % 16 for t in range(2)]

    def classes(n, st):
        return [(n, c0s[st] + m, 16 * (H - 1) + c0s[st] + m + 1, 16) for m in range(2)]

    def consts_v():
        fill(("o16", 0, 128), -0.0625)
        fill(("c32c", 0, 1), float(CAP))
        ts(("cki", 0, 512), ("col", 0, 512), 15, Op.bitwise_and)
        ts(("dg", 0, 256), ("cki", 0, 256), ("p15", 0, 1), Op.is_equal)
        for lo, hi in ((0, 512), (512, 1024)):
            ts(("seg", lo, hi), ("cki", 0, 512), 0.0, Op.is_gt)
        fill(("neg1", 0, 1), -1.0)
        fill(("half", 0, 1), 0.5)
        fill(("mbig", 0, 1), -3.0e7)

    def consts_v2():
        for t in range(1, ROUNDS):
            fill(("ln", BL * (4 * t + r), BL * (4 * t + r) + 4), 0.0)
        for n in ("e1", "ns1"):
            fill((n, L, LX), 0.0)
        for i in range(2):
            fill(("lv%d" % i, L, LX), float(V))
        fill(("qf0", L, LX), float(V))
        ts(("kp", 0, 512), ("cki", 0, 512), -512.0, Op.mult, 7680.0, Op.add)
        ts(("c32", 0, 64), ("col", 0, 64), 31, Op.bitwise_and)
        ts(("seg32", 0, 64), ("c32", 0, 64), 0.0, Op.is_gt)
        for c in range(2):
            ts(("dmp", c, c + 1), ("sc", c, c + 1), 576.0, Op.add)
            ts(("tri", 32 * c, 32 * c + 32), ("col", 0, 32), ("sc", c, c + 1), Op.is_lt, ("dmp", c, c + 1), Op.mult)
        for n in ("jwa", "jwb", "jwc"):
            ts((n, 0, 32), ("jwf", 0, 32), ("p15", 0, 1), Op.add)

    def consts_g():
        iota(("jwf", 0, 32), [[BL, 16], [16, 2]], 4, 0, True)
        iota(("en", 0, G0), [[0, G0]], 0, 0, True)
        iota(("rs", 0, G0), [[0, G0]], -SHIFT - 16384, 0, True)
        iota(("idc", 0, 512), [[BL, 16], [1, 32]], 4 - SHIFT, 0, True)
        iota(("w", 0, IDW), [[1, IDW]], -SHIFT, 0, True)
        iota(("vn", 0, G0), [[-1, G0]], V, 0, True)
        iota(("jt", 0, VT), [[1, VT]], 0, 0, True)
        iota(("vid", 0, IDW), [[0, IDW]], 0, 0, True)

    def names_again(st, lo, hi):
        act(("qr%d" % st, 16 * lo, 16 * hi), ("I", ("qf%d" % st, 0, LX), ("lrep", lo, hi)), Fn.Identity, ("c1280", 0, 1), -1.0)

    def consts_s():
        names_again(1, H, L)
        act(("i1280", 0, 128), ("idn", 0, 128), Fn.Copy, 0.0, 1280.0)
        act(("bd8", 0, 128), ("bd", 0, 128), Fn.Copy, 0.0, 8192.0)
        act(("kb", 0, 512), ("seg", 0, 512), Fn.Identity, ("mbig", 0, 1), 6.0e7)
        for k in range(16):
            act(("dk", 128 * k, 128 * k + 128), ("idn", 0, 128), Fn.Copy, 0.0, ("dg", k, k + 1))
        act(("idead", 0, 128), ("idn", 0, 128), Fn.Copy, 0.0, -32768.0)
        act(("ipen", 0, 128), ("idn", 0, 128), Fn.Copy, 0.0, -64.0)

    def sums(buf, lo, hi):
        for k in range(16):
            mm(("bdeg", lo, hi), ("idn", 0, 128), (buf, 16 * lo + k, 16 * (hi - 1) + k + 1, 16), k == 0, k == 15)

    def hits(t):
        st, old = t % 2, 4 * (t - 1)
        if t > 0:
            put("rs", old, old + 4, ("ksn", 0, 128))
        if t == 0:
            ts(("ok", 0, L), ("bdeg", 0, L), ("limf", 0, 1), Op.is_le)
        else:
            tt(("ok", 0, L), ("bdeg", 0, L), ("lmx", 0, L), Op.is_le)
        if t >= 2:
            mm(("bhit", 0, L), ("ipen", 0, 128), ("dead%d" % st, 0, L), True, False)
        mm(("bhit", 0, L), ("bd", 0, 128), ("ok", 0, L), t < 2, True)
        ts(("hit", 0, L), ("bhit", 0, L), 9.0, Op.is_ge)
        scan(("cum", 0, LX), ("hit", 0, LX), ("c255", 0, LX), Op.add, Op.min)
        for c in range(2):
            act(("sg", c * LX, (c + 1) * LX), ("cum", 0, LX), Fn.Sign, ("sh", c, c + 1), -1.0, ("pla", c, c + 1))
        if t == 0:
            ts(("deg", 0, L), ("bdeg", 0, L), -1.0, Op.mult, ("limf", 0, 1), Op.add)
        else:
            tt(("deg", 0, L), ("lmx", 0, L), ("bdeg", 0, L), Op.subtract)
        if t > 1:
            put("rs", 0, old, ("jr", 0, 32 * old))
        ts(("plw", 0, 2), ("pla", 0, 2), 0.5, Op.mult, float(LX // 2), Op.add)

    def variables(t):
        st, b = t % 2, 4 * t + r
        act(("vy", 0, 2), ("pla", 0, 2), Fn.Sign, ("c33", 0, 1))
        act(("vx", 0, 2), ("vy", 0, 2), Fn.Identity, ("kv%d" % st, 0, 1), (1 - V) / 2.0)
        for c in range(2):
            act(("la", BL * b + c, BL * b + c + 1), ("pla", c, c + 1), Fn.Identity, ("vx", c, c + 1), 8.0)

    def sizes(t):
        b = 4 * t + r
        ts(("la", BL * b + 4, BL * (b + 1)), ("I", ("deg", 0, LX), ("plw", 0, 2)), ("limb", 0, 1), Op.subtract, -256.0, Op.max)

    def dead_of(t):
        ts(("piv", 0, L), ("cum", 0, L), float(CAP), Op.is_le)
        tt(("dead%d" % t, 0, L), ("piv", 0, L), ("hit", 0, L), Op.mult)

    def count(t):
        act(("a1", 0, 1), ("cum", L - 1, L), Fn.Relu, ("c32c", 0, 1), -1.0)
        mm(("bhit", 0, 1), ("o16", 0, 128), ("a1", 0, 1), True, True)

    def limits(t):
        tc(("ai", 0, 1), ("bhit", 0, 1))
        ts(("aj", 0, 1), ("ai", 0, 1), 7, Op.bitwise_and)
        tt(("lima", 0, 1), ("limf", 0, 1), ("aj", 0, 1), Op.add)
        ts(("limb", 0, 1), ("lima", 0, 1), 1.0, Op.add)

    def list_v(b):
        tc(("evu", 2 * b, 2 * b + 2), ("la", BL * b, BL * b + 2))

    def list_c(b):
        tc(("cwu", 2 * b, 2 * b + 2), ("la", BL * b + 2, BL * b + 4))

    def put(table, lo, hi, src):
        tc(("I", (table, 0, VT), ("evu", 2 * lo, 2 * hi)), src)

    def put_names(b):
        o, i = ("I", ("nm", 0, VT), ("evu", 2 * b, 2 * b + 2)), ("ln", BL * b + 4, BL * (b + 1))
        ts(o, i, -1.0, Op.mult, float(V), Op.add)

    def size_of(b):
        i = 32 * (b % 4)
        act(("xt", i, i + 32), ("la", BL * b + 4, BL * (b + 1)), Fn.Identity, ("neg1", 0, 1), -1.0)

    def outputs(t):
        for q in range(N):
            b = 4 * t + q
            i = 32 * q
            act(("nt", i, i + 32), ("ln", BL * b + 4, BL * (b + 1)), Fn.Identity, ("c1280", 0, 1), -1.0)
            act(("vid", BL * b + 4, BL * (b + 1)), ("I", ("jt", 0, VT), ("evu", 2 * b, 2 * b + 2)))
        put("nm", 4 * t, 4 * t + 4, ("nt", 0, 128))
        put("xo", 4 * t, 4 * t + 4, ("xt", 0, 128))

    def picks(t):
        st = t % 2
        for lo, hi in CH:
            act(("xg", 16 * lo, 16 * hi), ("I", ("xm", 0, G0), ("qu%d" % st, lo, hi)))

    def self_picks():
        for k in range(16):
            mm(("bself", 0, L), ("dk", 128 * k, 128 * k + 128), ("xg", k, 16 * (L - 1) + k + 1, 16), k == 0, k == 15)

    def main(t):
        st, old = t % 2, 4 * (t - 1)

        def cover(c):
            lo, hi = CH[c]
            tt(("eq", 16 * lo, 16 * hi), ("I", ("en", 0, G0), ("qu%d" % st, lo, hi)), ("qr%d" % st, 16 * lo, 16 * hi), Op.is_equal)
            if t >= 2:
                mm((PSUM[c], 0, hi - lo), ("idead", 0, 128), ("dead%d" % st, lo, hi), True, False)
            for k in range(16):
                mm((PSUM[c], 0, hi - lo), ("i1280", 0, 128), ("eq", 16 * lo + k, 16 * (hi - 1) + k + 1, 16), t < 2 and k == 0, k == 15)

        def uncovered(c):
            lo, hi = CH[c]
            tt(("q2", lo, hi), ("qf%d" % st, lo, hi), (PSUM[c], 0, hi - lo), Op.max)
            ts(("qn", lo, hi), ("q2", lo, hi), float(V), Op.min)

        def pick(c, on):
            lo, hi = CH[c]
            o, i = ("xv", 16 * lo, 16 * hi), ("I", ("xm", 0, G0), ("qn", lo, hi))
            if on == "s":
                act(o, i, Fn.Relu)
            else:
                ts(o, i, 0.0, Op.max)

        def largest(c):
            lo, hi = CH[c]
            scan(("msc", 16 * lo, 16 * hi), ("seg", 0, 16 * (hi - lo)), ("xg", 16 * lo, 16 * hi), Op.mult, Op.min)

        cover(0)
        tt(("ksn", 0, 128), ("idc", 32 * old, 32 * old + 128), ("bkey", 0, 128), Op.add)
        cover(1)
        uncovered(0)
        pick(0, "s")
        cover(2)
        uncovered(1)
        pick(1, "s")
        sums("xv", *CH[0])
        largest(0)
        uncovered(2)
        pick(2, "v")
        largest(1)
        largest(2)
        ts(("lmx", 0, L), ("msc", 15, 16 * L, 16), ("limb", 0, 1), Op.add, ("lima", 0, 1), Op.min)
        for q in range(N):
            act(("ksl", BL * (old + q) + 4, BL * (old + q + 1)), ("ksn", 32 * q, 32 * q + 32))
        if t > 1:
            act(("jr", 0, 32 * old), ("I", ("ksl", 0, BL * (old + 4)), (("jwb", "jwc")[t - 2], 0, 2 * old)))
        for c in range(2):
            tc(("evu", 2 * old + c, 2 * old + 7 + c, 2), ("la", BL * old + c, BL * (old + 3) + c + 1, BL))
        sums("xv", *CH[2])
        sums("xv", *CH[1])

    def pivots(t):
        st, b = t % 2, 4 * t + r

        def keys():
            tt(("key", 0, 512), ("I", ("rs", 0, G0), ("qp", 0, 32)), ("kp", 0, 512), Op.add)
            scan(("ksc", 0, 512), ("kb", 0, 512), ("key", 0, 512), Op.min, Op.max)

        def own_gathers():
            self_picks()
            act(("esg", 0, L), ("bself", 0, L), Fn.Sign, ("half", 0, 1))
            act(("e1", 0, L), ("esg", 0, L), Fn.Relu, 0.0, float(V))
            act(("ocx", 0, L), ("q2", 0, L), Fn.Identity, ("c1280", 0, 1), -1.0)
            act(("e1p", 0, 32), ("I", ("e1", 0, LX), ("plw", 0, 2)))

        def names():
            tt(("b0", 0, 512), ("xn", 0, 512), ("b1", 0, 512), Op.not_equal)
            tt(("cc", 0, 512), ("xn", 0, 512), ("b0", 0, 512), Op.mult)
            scan(("nsc", 0, 512), ("seg", 0, 512), ("cc", 0, 512), Op.mult, Op.max)
            tt(("ocp", 0, 32), ("I", ("ocx", 0, LX), ("plw", 0, 2)), ("e1p", 0, 32), Op.min)
            tt(("ocq", 0, 32), ("I", ("ns%d" % st, 0, LX), ("plw", 0, 2)), ("ocp", 0, 32), Op.mult)
            tt(("ln", BL * b + 4, BL * (b + 1)), ("ocq", 0, 32), ("nsc", 15, 512, 16), Op.max)
            send(b, [("ln", "n")])

        def claims():
            tc(("mi", 0, 32), ("ksc", 15, 512, 16))
            ts(("mj", 0, 32), ("mi", 0, 32), 511, Op.bitwise_and)
            tt(("kd", 0, 32), ("mj", 0, 32), ("dg", 0, 32), Op.mult)
            scan(("kw", 0, 32), ("seg", 0, 32), ("kd", 0, 32), Op.mult, Op.add)
            for c in range(2):
                ts(("ke", 32 * c, 32 * c + 32), ("mj", 0, 32), ("kw", 16 * c + 15, 16 * c + 16), Op.is_equal)
            tt(("kf", 0, 64), ("ke", 0, 64), ("tri", 0, 64), Op.mult)
            scan(("kg", 0, 64), ("seg32", 0, 64), ("kf", 0, 64), Op.mult, Op.max)
            tt(("la", BL * b + 2, BL * b + 4), ("kw", 15, 32, 16), ("kg", 31, 64, 32), Op.max)
            send(b, [("la", "a")])

        tc(("qp", 0, 32), ("I", ("qf%d" % st, 0, LX), ("plw", 0, 2)))
        act(("xn", 0, 512), ("I", ("en", 0, G0), ("qp", 0, 32)))
        keys()
        tc(("vp", 0, 32), ("I", ("lv%d" % st, 0, LX), ("plw", 0, 2)))
        variables(t)
        if t < ROUNDS - 1:
            count(t)
        act(("vr", 0, 512), ("I", ("vn", 0, G0), ("vp", 0, 32)))
        act(("b1", 0, 512), ("vr", 0, 512))
        own_gathers()
        sizes(t)
        claims()
        if t < ROUNDS - 1:
            limits(t)
        if t < 2:
            dead_of(t)
        names()

    def kept_rows(t):
        st = t % 2
        tt(("b1", 0, L), ("qf%d" % st, 0, L), ("e1", 0, L), Op.max)
        if t == 1:
            tt(("qf1", 0, L), ("q2", 0, L), ("b1", 0, L), Op.min)
            tc(("qu1", 0, L), ("qf1", 0, L))
        else:
            tt(("q3", 0, L), ("q2", 0, L), ("b1", 0, L), Op.min)
            for m, x in enumerate(classes("nm", st)):
                act(x, ("q3", m * H, (m + 1) * H))

    def update(t):
        jo, jn = (None, "jwa", "jwb")[t], (None, "jwb", "jwc")[t]
        old = 4 * t
        n = 32 * old

        def place(table, b, src):
            tc(("I", (table, 0, VT), ("vc", 4 * b, 4 * b + 2)), src)

        def land(qs, lists, sz, nms):
            for q in qs:
                b = 4 * t + q
                if lists:
                    tc(("vc", 4 * b, 4 * b + 4), ("la", BL * b, BL * b + 4))
                    size_of(b)
                if sz:
                    place("xm", b, ("la", BL * b + 4, BL * (b + 1)))
                if nms:
                    place("en", b, ("ln", BL * b + 4, BL * (b + 1)))

        land(first, True, True, False)
        land(first, False, False, True)
        land(last, True, t == 0, False)
        mm(("bkey", 0, 128), ("bd8", 0, 128), ("xt", 0, 128), True, True)
        if t > 0:
            for q in (3, 2, 1, 0):
                b = 4 * t + q
                tc(("I", ("w", 0, IDW), ("vc", 4 * b + 2, 4 * b + 4)), ("idc", 32 * b, 32 * b + 32))
            tt(("jd", 0, n), ("I", ("w", 0, IDW), (jo, 0, 2 * old)), ("dg", 0, n), Op.mult)
            scan(("js", 0, n), ("seg", 0, n), ("jd", 0, n), Op.mult, Op.add)
            ts((jn, 0, 2 * old), ("js", 15, n, 16), float(SHIFT), Op.add)
            act(("xr", 0, n), ("I", ("la", 0, BL * (old + 4)), (jn, 0, 2 * old)))
            land(last, False, True, False)
            put("xm", 0, old, ("xr", 0, n))
        picks(t + 1)
        land(last, False, False, True)
        if t > 0:
            tc(("er", 0, n), ("I", ("ln", 0, BL * (old + 4)), (jn, 0, 2 * old)))
            put("en", 0, old, ("er", 0, n))

    dma("y", T["nm"][:, 0:V], T.nb[:, :], "dn", [], [("nm", 0, V)])
    dma("s", T["xm"][:, 0:V], T.xs[:, :], "dx", [], [("xm", 0, V)])
    dma("s", T["limi"][:, 0:1], T.lim[:, 0:1], "dl", [], [("limi", 0, 1)])
    wait_for("y", [("dn", 16, {})])
    dma("y", T["xo"][:, 0:V], T.xs[:, :], "do", [], [("xo", 0, V)])
    iota(("pii", 0, 1), [[1, 1]], 0, 1)
    iota(("col", 0, 512), [[1, 512]], 0, 0)
    fill(("one", 0, 128), 1.0)
    emit("g", lambda: g.affine_select(T["idn"][:, :], T["one"][:, :], [[-1, 128]], Op.is_equal, 0.0, 0, 1),
         [("idn", 0, 128)], [("one", 0, 128)])
    for i in range(2):
        iota(("lv%d" % i, 0, L), [[1, 2], [16, H]], c0s[i], 0, True)
    fill(("xm", V, V + 16), 0.0)
    fill(("hit", L, LX), 1.0)
    fill(("c255", 0, LX), 255.0)
    for n in ("deg", "ocx", "ns0"):
        fill((n, L, LX), 0.0)
    fill(("qf1", L, LX), float(V))
    fill(("c1280", 0, 1), float(V))
    fill(("ksl", 0, 576), 0.0)
    fill(("c33", 0, 1), float(LX - 2 * H + 1))
    for i in range(2):
        fill(("kv%d" % i, 0, 1), 8.0 * LX + c0s[i] + (1 - V) / 2.0)
    ts(("pij", 0, 1), ("pii", 0, 1), 15, Op.bitwise_and)
    ts(("pij", 1, 2), ("pii", 0, 1), 4, Op.arith_shift_right)
    tc(("p15", 0, 1), ("pij", 0, 1))
    tc(("pg", 0, 1), ("pij", 1, 2))
    for c in range(2):
        ts(("sc", c, c + 1), ("p15", 0, 1), 16.0 * c, Op.add)
        ts(("sh", c, c + 1), ("p15", 0, 1), 16.0 * c + 0.5, Op.add)
    ts(("gi", 0, 128), ("col", 0, 128), 4, Op.arith_shift_right)
    ts(("bd", 0, 128), ("gi", 0, 128), ("pg", 0, 1), Op.is_equal)
    for buf in ("la", "ln"):
        fill((buf, BL * r, BL * r + 4), 0.0)
    tc(("lrep", 0, L), ("col", 0, L))
    tc(("limf", 0, 1), ("limi", 0, 1))
    ts(("limb", 0, 1), ("limf", 0, 1), 1.0, Op.add)

    for m, x in enumerate(classes("nm", 0)):
        tc(("qu0", m * H, (m + 1) * H), x)
    for lo, hi in CH0:
        mid = (lo + hi) // 2
        for f, a, z in ((tc, lo, mid), (act, mid, hi)):
            f(("xv", 16 * a, 16 * z), ("I", ("xm", 0, G0), ("qu0", a, z)))
        sums("xv", lo, hi)
    for st in (1, 0):
        for m, x in enumerate(classes("nm", st)):
            tc(("qf%d" % st, m * H, (m + 1) * H), x)
    act(("ocx", 0, L), ("qf0", 0, L), Fn.Identity, ("c1280", 0, 1), -1.0)
    names_again(1, 0, H)
    tc(("qu1", 0, L), ("qf1", 0, L))
    tt(("ns0", 0, L), ("qf0", 0, L), ("lv0", 0, L), Op.not_equal)
    hits(0)
    sizes(0)
    variables(0)
    tc(("ocp", 0, 32), ("I", ("ocx", 0, LX), ("plw", 0, 2)))
    tt(("ln", BL * r + 4, BL * (r + 1)), ("I", ("ns0", 0, LX), ("plw", 0, 2)), ("ocp", 0, 32), Op.mult)
    send(r, [("la", "a"), ("ln", "n")])
    consts_g()
    consts_v()
    count(0)
    limits(0)
    consts_s()
    dead_of(0)
    tt(("ns1", 0, L), ("qf1", 0, L), ("lv1", 0, L), Op.not_equal)
    consts_v2()
    update(0)

    for t in range(1, ROUNDS):
        main(t)
        hits(t)
        pivots(t)
        outputs(t - 1)
        if t == 1:
            for lo, hi in CH:
                names_again(0, lo, hi)
        kept_rows(t)
        if t > 1:
            put_names(4 * (t - 2) + r)
        if t < ROUNDS - 1:
            update(t)

    t, old = 3, 12

    def lands(qs):
        for q in qs:
            b = 4 * t + q
            list_v(b)
            act(("vb", 32 * q, 32 * q + 32), ("I", ("jt", 0, VT), ("evu", 2 * b, 2 * b + 2)))
            size_of(b)
            list_c(b)

    def sizes_out(qs):
        for q in qs:
            put("xo", 12 + q, 13 + q, ("xt", 32 * q, 32 * q + 32))

    lands(first)
    sizes_out(first)
    for q in first:
        put_names(12 + q)
    lands(last)
    for q in (3, 2, 1, 0):
        tc(("I", ("vid", 0, IDW), ("cwu", 24 + 2 * q, 26 + 2 * q)), ("vb", 32 * q, 32 * q + 32))
    for lo, hi in ((0, 8), (8, old)):
        act(("jf", 32 * lo, 32 * hi), ("I", ("vid", 0, IDW), ("jwc", 2 * lo, 2 * hi)))
    sizes_out(last)
    dma("s", T.yx[:, :], T["xo"][:, 0:V], "ox", [("xo", 0, V)], [])
    for q in last:
        put_names(12 + q)
    dma("y", T.yn[:, :], T["nm"][:, 0:V], "on", [("nm", 0, V)], [])
    put("jt", 0, 8, ("jf", 0, 256))
    put("jt", 8, old, ("jf", 256, 384))
    dma("y", T.yj[:, :], T["jt"][0:128:16, 0:V], "oj", [("jt", 0, V)], [])
    for s, v in totals.items():
        if known["g"].get(s, 0) < v:
            g.wait_ge(T.sem[s], v)
